import numpy as np
import ml_dtypes


def mxq(x, axis, fmt="e4m3"):
    dtype, down = {"e4m3": (ml_dtypes.float8_e4m3fn, 7), "e5m2": (ml_dtypes.float8_e5m2, 14)}[fmt]
    v = np.moveaxis(np.asarray(x, np.float32).astype(ml_dtypes.bfloat16).astype(np.float64), axis, -1)
    blocks = v.reshape(v.shape[:-1] + (-1, 32))
    amax = np.abs(blocks).max(-1, keepdims=True)
    byte = np.maximum(np.where(amax > 0, np.frexp(amax)[1] - 1 + 127, 0) - down, 1)
    scale = np.exp2(byte - 127.0)
    codes = (blocks / scale).astype(np.float32).astype(dtype).astype(np.float64)
    return np.moveaxis((codes * scale).reshape(v.shape), -1, axis)


WIDE = False


def mx_kscale(k):
    if not WIDE:
        return np.ones(k)
    levels = np.array([10, -10, 5, -5, 0])
    if k % 512:
        return np.exp2(np.random.permutation(np.resize(levels, k // 32))).repeat(32)
    a = np.empty((k // 512, 16))
    for p in range(k // 512):
        a[p, :8] = np.random.permutation(np.resize(levels, 8))
        for g in range(8):
            far = levels[np.abs(levels - a[p, g]) >= 10]
            a[p, g + 8] = far[np.random.randint(len(far))]
    return np.exp2(a.ravel()).repeat(32)


def f64(x):
    return np.asarray(x).astype(np.float64)


def striped(idx):
    return np.tile(idx.reshape(-1, 16).T, (8, 1)).astype(np.uint16)


def unstriped(offs):
    return offs[:16].T.reshape(-1).astype(np.int64)


E2M1 = np.array([0.0, 0.5, 1.0, 1.5, 2.0, 3.0, 4.0, 6.0, -0.0, -0.5, -1.0, -1.5, -2.0, -3.0, -4.0, -6.0])


def pack_weight(w, fmt):
    k, n = w.shape
    w = f64(np.asarray(w, np.float32).astype(ml_dtypes.bfloat16)).reshape(k // 32, 32, n)
    amax = np.abs(w).max(1)
    if fmt == "e4m3":
        byte = np.frexp(amax)[1] - 1 + 127 - 7
    else:
        mant, ex = np.frexp(amax / 6.0)
        byte = np.where(mant > 0.5, ex, ex - 1) + 127
    byte = np.clip(np.where(amax > 0, byte, 1), 1, 254)
    scaled = (w * np.exp2(127.0 - byte)[:, None, :]).reshape(k, n).astype(np.float32)
    by_word = np.ascontiguousarray(scaled.reshape(k // 512, 128, 4, n).transpose(0, 1, 3, 2))
    if fmt == "e4m3":
        words = by_word.astype(ml_dtypes.float8_e4m3fn).view(np.uint8)
    else:
        c = by_word.astype(ml_dtypes.float4_e2m1fn).view(np.uint8) & 0xF
        words = (c[..., 0::2] | (c[..., 1::2] << 4)).reshape(k // 512, 128, 2 * n)
    return np.ascontiguousarray(words), np.ascontiguousarray(byte.astype(np.uint8).reshape(k // 512, 16, n))


def unpack_weight(words, scales, fmt):
    g, _, n = scales.shape
    words = np.ascontiguousarray(words).reshape(g, 128, n, -1)
    if fmt == "e4m3":
        vals = words.view(ml_dtypes.float8_e4m3fn).astype(np.float64)
    else:
        nib = np.empty((g, 128, n, 4), np.uint8)
        nib[..., 0::2] = words & 0xF
        nib[..., 1::2] = words >> 4
        vals = E2M1[nib]
    vals = vals * np.repeat(np.exp2(scales.astype(np.float64) - 127.0), 8, axis=1)[..., None]
    return vals.transpose(0, 1, 3, 2).reshape(g * 512, n)


def gelu(v):
    return 0.5 * v * (1.0 + np.tanh(np.sqrt(2.0 / np.pi) * (v + 0.044715 * v**3)))


K, H, N, T, S = 512, 1536, 512, 2048, 1024

def setup_inputs():
    n = np.random.standard_normal
    s = mx_kscale(K)[:, None]
    u = mx_kscale(H)[:, None]
    tab_words, tab_scales = pack_weight(n((K, T)) * s, "e4m3")
    wg_words, wg_scales = pack_weight(n((K, H)) / np.sqrt(K) / s, "e2m1")
    wu = (n((K, H)) / np.sqrt(K) / s * u.T).astype(np.float32)
    wd_words, wd_scales = pack_weight(n((H, N)) / np.sqrt(H) / u, "e4m3")
    bg = (0.5 * n(H)).astype(np.float32)
    gT = n((N, T)).astype(np.float32)
    offs = striped(np.random.permutation(T)[:S])
    return {"tab_words": tab_words, "tab_scales": tab_scales, "offs": offs,
            "wg_words": wg_words, "wg_scales": wg_scales, "wu": wu,
            "wd_words": wd_words, "wd_scales": wd_scales, "bg": bg, "gT": gT}

def reference(tab_words, tab_scales, offs, wg_words, wg_scales, wu, wd_words, wd_scales, bg, gT):
    v = unpack_weight(tab_words, tab_scales, "e4m3")[:, unstriped(offs)]
    wg = unpack_weight(wg_words, wg_scales, "e2m1")
    wd = unpack_weight(wd_words, wd_scales, "e4m3")
    g = f64(gT)[:, unstriped(offs)]
    a = (wg.T @ v) + f64(bg)[:, None]
    b = mxq(f64(wu), 0, "e4m3").T @ v
    h = a / (1.0 + np.exp(-a)) * b
    y = wd.T @ mxq(h, 0, "e4m3")
    out = y + g
    return out

@@ -1,0 +1,211 @@
+from contextlib import ExitStack
+
+import concourse.mybir as mybir
+
+K, H, N, T, S = 512, 1536, 512, 2048, 1024
+FLOPS = 2 * S * H * (2 * K + N)
+
+F32 = mybir.dt.float32
+BF16 = mybir.dt.bfloat16
+I32 = mybir.dt.int32
+U32 = mybir.dt.uint32
+U16 = mybir.dt.uint16
+U8 = mybir.dt.uint8
+FP8X4 = mybir.dt.float8_e4m3fn_x4
+FP4X4 = mybir.dt.float4_e2m1fn_x4
+ADD = mybir.AluOpType.add
+MULT = mybir.AluOpType.mult
+SILU = mybir.ActivationFunctionType.Silu
+
+P = 128
+PACK = 4
+PASS = P * PACK
+R_BLOCKS = H // PASS
+N_TILES = N // P
+HALF = S // 2
+CHUNK = 128
+RUN = 4
+
+
+def load_scale_rows(queue, plane, rows):
+    for q in range(4):
+        queue.dma_start(out=plane[32 * q : 32 * q + 4], in_=rows[4 * q : 4 * q + 4])
+
+
+def tile_list_paged_swiglu_residual_kernel(
+    tc, tab_words, tab_scales, offs, wg_words, wg_scales, wu, wd_words, wd_scales, bg, gT, out
+):
+    nc = tc.nc
+    with ExitStack() as ctx:
+        keep = ctx.enter_context(tc.tile_pool(name="keep", bufs=1))
+        work = ctx.enter_context(tc.tile_pool(name="work", bufs=2))
+        psum = ctx.enter_context(tc.psum_pool(name="psum", bufs=1))
+
+        offsets = keep.tile([P, S // 16], U16, name="offsets")
+        nc.sync.dma_start(offsets[:], offs)
+
+        tab_plane = keep.tile([P, T // 4], I32, name="tab_plane", align_bytes=64)
+        nc.vector.memset(tab_plane[:], 0)
+        wg_plane_raw = keep.tile([P, H // 4], I32, name="wg_plane_raw", align_bytes=64)
+        nc.vector.memset(wg_plane_raw[:], 0)
+        wd_plane = keep.tile([P, R_BLOCKS, N // 4], I32, name="wd_plane", align_bytes=64)
+        nc.vector.memset(wd_plane[:], 0)
+
+        bias = keep.tile([P, R_BLOCKS, PACK], F32, name="bias")
+        nc.sync.dma_start(out=bias[:], in_=bg.rearrange("(a p t) -> p a t", p=P, t=PACK))
+        load_scale_rows(nc.sync, tab_plane, tab_scales[0].bitcast(I32))
+        tab_codes = keep.tile([P, T], I32, name="tab_codes", align_bytes=64)
+        nc.sync.dma_start(out=tab_codes[:], in_=tab_words[0].rearrange("p t i -> p (t i)").bitcast(I32))
+        wg_raw = keep.tile([P, H // 2], I32, name="wg_raw", align_bytes=64)
+        nc.sync.dma_start(out=wg_raw[:], in_=wg_words[0].bitcast(I32))
+        load_scale_rows(nc.sync, wg_plane_raw, wg_scales[0].bitcast(I32))
+
+        def load_up_weight(a):
+            raw = keep.tile([P, PACK * PASS], F32, name=f"wu_raw{a}")
+            nc.sync.dma_start(
+                out=raw[:].rearrange("p (j c) -> p j c", j=PACK),
+                in_=wu[:, a * PASS : (a + 1) * PASS].rearrange("(p j) c -> p j c", j=PACK),
+            )
+            return raw
+
+        wu_raw = [load_up_weight(0), load_up_weight(1)]
+        load_scale_rows(nc.sync, wd_plane, wd_scales.bitcast(I32).rearrange("a q c -> q a c"))
+        wd_codes = keep.tile([P, R_BLOCKS, N], I32, name="wd_codes", align_bytes=64)
+        nc.sync.dma_start(out=wd_codes[:], in_=wd_words.rearrange("a p c i -> p a (c i)").bitcast(I32))
+        wu_raw.append(load_up_weight(2))
+
+        residual_rows = []
+        for n in range(N_TILES):
+            g_rows = keep.tile([P, T], F32, name=f"g_rows{n}")
+            nc.sync.dma_start(out=g_rows[:], in_=gT[n * P : (n + 1) * P, :])
+            residual_rows.append(g_rows)
+
+        def half_list(h):
+            cols = HALF // 16
+            return offsets[:, h * cols : (h + 1) * cols]
+
+        def gather_states(h):
+            plane = keep.tile([P, HALF], U8, name=f"v_plane{h}", align_bytes=64)
+            nc.vector.tensor_copy(plane[:], tab_plane[:].bitcast(U8).indirect(half_list(h)))
+            codes = keep.tile([P, HALF], U32, name=f"v_codes{h}", align_bytes=64)
+            nc.vector.tensor_copy(codes[:], tab_codes[:].bitcast(U32).indirect(half_list(h)))
+            return codes, plane
+
+        def reorder_gate_weight(a):
+            cols = slice(a * PASS, (a + 1) * PASS)
+            codes = keep.tile([P, PASS], U16, name=f"wg_codes{a}", align_bytes=64)
+            nc.vector.tensor_copy(
+                out=codes[:].rearrange("p (t m) -> p t m", t=PACK),
+                in_=wg_raw[:].bitcast(U16)[:, cols].rearrange("p (m t) -> p t m", t=PACK),
+            )
+            plane = keep.tile([P, PASS], U8, name=f"wg_plane{a}", align_bytes=64)
+            nc.vector.tensor_copy(
+                out=plane[:].rearrange("p (t m) -> p t m", t=PACK),
+                in_=wg_plane_raw[:].bitcast(U8)[:, cols].rearrange("p (m t) -> p t m", t=PACK),
+            )
+            return codes, plane
+
+        def quantize_up_weight(a):
+            grouped = work.tile([P, PASS * PACK], BF16, name="wu_grouped", align_bytes=64)
+            dst = grouped[:].rearrange("p (t m j) -> p m j t", t=PACK, j=PACK)
+            src = wu_raw[a][:].rearrange("p (j m t) -> p m j t", j=PACK, t=PACK)
+            if a == 0:
+                nc.vector.tensor_copy(out=dst, in_=src)
+            else:
+                nc.scalar.copy(out=dst, in_=src)
+            codes = keep.tile([P, PASS], U32, name=f"wu_codes{a}", align_bytes=64)
+            plane = keep.tile([P, PASS], U8, name=f"wu_plane{a}", align_bytes=64)
+            nc.vector.quantize_mx(out=codes[:].bitcast(FP8X4), scales=plane[:], in_=grouped[:])
+            return codes, plane
+
+        def gate(a, wg_mx, v_mx):
+            gated = work.tile([P, PACK, HALF], F32, name="gated", bufs=3)
+            for t in range(PACK):
+                bank = psum.tile([P, HALF], F32, name="gate_bank", bufs=2)
+                nc.tensor.matmul_mx(
+                    out=bank[:],
+                    lhsT=wg_mx[0][:].bitcast(U8)[:, 2 * P * t : 2 * P * (t + 1)].bitcast(FP4X4),
+                    lhsT_scale=wg_mx[1][:, P * t : P * (t + 1)],
+                    rhs=v_mx[0][:].bitcast(FP8X4),
+                    rhs_scale=v_mx[1][:],
+                    start=True,
+                    stop=True,
+                )
+                nc.scalar.activation(out=gated[:, t, :], in_=bank[:], func=SILU, bias=bias[:, a, t : t + 1])
+            return gated
+
+        def up_and_product(gated, wu_mx, v_mx):
+            hidden = work.tile([P, HALF * PACK], BF16, name="hidden", align_bytes=64)
+            for c in range(HALF // CHUNK):
+                tokens = slice(c * CHUNK, (c + 1) * CHUNK)
+                bank = psum.tile([P, PACK, CHUNK], F32, name="up_bank", bufs=2)
+                for t in range(PACK):
+                    nc.tensor.matmul_mx(
+                        out=bank[:, t, :],
+                        lhsT=wu_mx[0][:, P * t : P * (t + 1)].bitcast(FP8X4),
+                        lhsT_scale=wu_mx[1][:, P * t : P * (t + 1)],
+                        rhs=v_mx[0][:, tokens].bitcast(FP8X4),
+                        rhs_scale=v_mx[1][:, tokens],
+                        start=True,
+                        stop=True,
+                    )
+                nc.vector.tensor_tensor(
+                    out=hidden[:, c * CHUNK * PACK : (c + 1) * CHUNK * PACK].rearrange(
+                        "p (g i t) -> p g t i", i=RUN, t=PACK
+                    ),
+                    in0=bank[:].rearrange("p t (g i) -> p g t i", i=RUN),
+                    in1=gated[:, :, tokens].rearrange("p t (g i) -> p g t i", i=RUN),
+                    op=MULT,
+                )
+            codes = work.tile([P, HALF], U32, name="h_codes", align_bytes=64)
+            plane = work.tile([P, HALF], U8, name="h_plane", align_bytes=64)
+            nc.vector.quantize_mx(out=codes[:].bitcast(FP8X4), scales=plane[:], in_=hidden[:])
+            return codes, plane
+
+        def down(a, h_mx, sums):
+            for n in range(N_TILES):
+                nc.tensor.matmul_mx(
+                    out=sums[n][:],
+                    lhsT=wd_codes[:, a, P * n : P * (n + 1)].bitcast(FP8X4),
+                    lhsT_scale=wd_plane[:, a, :].bitcast(U8)[:, P * n : P * (n + 1)],
+                    rhs=h_mx[0][:].bitcast(FP8X4),
+                    rhs_scale=h_mx[1][:],
+                    start=(a == 0),
+                    stop=(a == R_BLOCKS - 1),
+                )
+
+        def store(h, n, result):
+            nc.sync.dma_start(out=out[n * P : (n + 1) * P, h * HALF : (h + 1) * HALF], in_=result[:])
+
+        v_mx = [gather_states(0)]
+        wg_mx = [reorder_gate_weight(0)]
+        wu_mx = [quantize_up_weight(0)]
+        picked = []
+        for h in range(2):
+            sums = [psum.tile([P, HALF], F32, name=f"down_bank{n}") for n in range(N_TILES)]
+            for a in range(R_BLOCKS):
+                gated = gate(a, wg_mx[a], v_mx[h])
+                if h == 0 and a + 1 < R_BLOCKS:
+                    wg_mx.append(reorder_gate_weight(a + 1))
+                    wu_mx.append(quantize_up_weight(a + 1))
+                down(a, up_and_product(gated, wu_mx[a], v_mx[h]), sums)
+                if h == 0 and a == 0:
+                    v_mx.append(gather_states(1))
+            if h == 0:
+                for n in range(N_TILES):
+                    product = keep.tile([P, HALF], F32, name=f"product{n}")
+                    nc.scalar.copy(out=product[:], in_=sums[n][:])
+                    g_picked = keep.tile([P, HALF], F32, name=f"picked{n}")
+                    nc.vector.tensor_copy(g_picked[:], residual_rows[n][:].indirect(half_list(1)))
+                    picked.append((product, g_picked))
+            else:
+                for n in range(N_TILES):
+                    result = keep.tile([P, HALF], F32, name=f"result0_{n}")
+                    nc.vector.tensor_tensor(
+                        result[:], residual_rows[n][:].indirect(half_list(0)), picked[n][0][:], ADD
+                    )
+                    store(0, n, result)
+                for n in range(N_TILES):
+                    result = keep.tile([P, HALF], F32, name=f"result1_{n}")
+                    nc.vector.tensor_tensor(out=result[:], in0=sums[n][:], in1=picked[n][1][:], op=ADD)
+                    store(1, n, result)

@@ -24,7 +24,7 @@ R_BLOCKS = H // PASS
 N_TILES = N // P
 HALF = S // 2
 CHUNK = 128
-RUN = 4
+RUN = 2
 
 
 def load_scale_rows(queue, plane, rows):
@@ -46,7 +46,7 @@ def tile_list_paged_swiglu_residual_kernel(
 
         tab_plane = keep.tile([P, T // 4], I32, name="tab_plane", align_bytes=64)
         nc.vector.memset(tab_plane[:], 0)
-        wg_plane_raw = keep.tile([P, H // 4], I32, name="wg_plane_raw", align_bytes=64)
+        wg_plane_raw = keep.tile([P, H // 4], I32, name="wg_plane_raw", tag="wg_plane_raw", align_bytes=64)
         nc.vector.memset(wg_plane_raw[:], 0)
         wd_plane = keep.tile([P, R_BLOCKS, N // 4], I32, name="wd_plane", align_bytes=64)
         nc.vector.memset(wd_plane[:], 0)
@@ -68,17 +68,18 @@ def tile_list_paged_swiglu_residual_kernel(
             )
             return raw
 
+        def load_residual_rows(n):
+            g_rows = keep.tile([P, T], F32, name=f"g_rows{n}")
+            nc.sync.dma_start(out=g_rows[:], in_=gT[n * P : (n + 1) * P, :])
+            return g_rows
+
         wu_raw = [load_up_weight(0), load_up_weight(1)]
+        residual_rows = [load_residual_rows(0)]
+        wu_raw.append(load_up_weight(2))
+        residual_rows.extend(load_residual_rows(n) for n in range(1, N_TILES))
         load_scale_rows(nc.sync, wd_plane, wd_scales.bitcast(I32).rearrange("a q c -> q a c"))
         wd_codes = keep.tile([P, R_BLOCKS, N], I32, name="wd_codes", align_bytes=64)
         nc.sync.dma_start(out=wd_codes[:], in_=wd_words.rearrange("a p c i -> p a (c i)").bitcast(I32))
-        wu_raw.append(load_up_weight(2))
-
-        residual_rows = []
-        for n in range(N_TILES):
-            g_rows = keep.tile([P, T], F32, name=f"g_rows{n}")
-            nc.sync.dma_start(out=g_rows[:], in_=gT[n * P : (n + 1) * P, :])
-            residual_rows.append(g_rows)
 
         def half_list(h):
             cols = HALF // 16
@@ -87,7 +88,7 @@ def tile_list_paged_swiglu_residual_kernel(
         def gather_states(h):
             plane = keep.tile([P, HALF], U8, name=f"v_plane{h}", align_bytes=64)
             nc.vector.tensor_copy(plane[:], tab_plane[:].bitcast(U8).indirect(half_list(h)))
-            codes = keep.tile([P, HALF], U32, name=f"v_codes{h}", align_bytes=64)
+            codes = keep.tile([P, HALF], U32, name=f"v_codes{h}", tag=("v_codes0", "wg_plane_raw")[h], align_bytes=64)
             nc.vector.tensor_copy(codes[:], tab_codes[:].bitcast(U32).indirect(half_list(h)))
             return codes, plane
 
@@ -121,7 +122,7 @@ def tile_list_paged_swiglu_residual_kernel(
         def gate(a, wg_mx, v_mx):
             gated = work.tile([P, PACK, HALF], F32, name="gated", bufs=3)
             for t in range(PACK):
-                bank = psum.tile([P, HALF], F32, name="gate_bank", bufs=2)
+                bank = psum.tile([P, HALF], F32, name="wide_bank", bufs=4)
                 nc.tensor.matmul_mx(
                     out=bank[:],
                     lhsT=wg_mx[0][:].bitcast(U8)[:, 2 * P * t : 2 * P * (t + 1)].bitcast(FP4X4),
@@ -138,7 +139,7 @@ def tile_list_paged_swiglu_residual_kernel(
             hidden = work.tile([P, HALF * PACK], BF16, name="hidden", align_bytes=64)
             for c in range(HALF // CHUNK):
                 tokens = slice(c * CHUNK, (c + 1) * CHUNK)
-                bank = psum.tile([P, PACK, CHUNK], F32, name="up_bank", bufs=2)
+                bank = psum.tile([P, PACK, CHUNK], F32, name="up_bank", bufs=4)
                 for t in range(PACK):
                     nc.tensor.matmul_mx(
                         out=bank[:, t, :],
@@ -157,55 +158,58 @@ def tile_list_paged_swiglu_residual_kernel(
                     in1=gated[:, :, tokens].rearrange("p t (g i) -> p g t i", i=RUN),
                     op=MULT,
                 )
-            codes = work.tile([P, HALF], U32, name="h_codes", align_bytes=64)
-            plane = work.tile([P, HALF], U8, name="h_plane", align_bytes=64)
+            codes = work.tile([P, HALF], U32, name="h_codes", bufs=2 * R_BLOCKS, align_bytes=64)
+            plane = work.tile([P, HALF], U8, name="h_plane", bufs=2 * R_BLOCKS, align_bytes=64)
             nc.vector.quantize_mx(out=codes[:].bitcast(FP8X4), scales=plane[:], in_=hidden[:])
             return codes, plane
 
-        def down(a, h_mx, sums):
-            for n in range(N_TILES):
+        def down(n, h_mx):
+            bank = psum.tile([P, HALF], F32, name="wide_bank", bufs=4)
+            for a in range(R_BLOCKS):
                 nc.tensor.matmul_mx(
-                    out=sums[n][:],
+                    out=bank[:],
                     lhsT=wd_codes[:, a, P * n : P * (n + 1)].bitcast(FP8X4),
                     lhsT_scale=wd_plane[:, a, :].bitcast(U8)[:, P * n : P * (n + 1)],
-                    rhs=h_mx[0][:].bitcast(FP8X4),
-                    rhs_scale=h_mx[1][:],
+                    rhs=h_mx[a][0][:].bitcast(FP8X4),
+                    rhs_scale=h_mx[a][1][:],
                     start=(a == 0),
                     stop=(a == R_BLOCKS - 1),
                 )
+            return bank
 
         def store(h, n, result):
             nc.sync.dma_start(out=out[n * P : (n + 1) * P, h * HALF : (h + 1) * HALF], in_=result[:])
 
+        def pick_residual(n):
+            g_picked = keep.tile([P, HALF], F32, name=f"picked{n}")
+            nc.vector.tensor_copy(g_picked[:], residual_rows[n][:].indirect(half_list(1)))
+            return g_picked
+
+        def finish_first_half(n):
+            product = keep.tile([P, HALF], F32, name=f"product{n}")
+            nc.scalar.copy(out=product[:], in_=down(n, h_mx[0])[:])
+            result = keep.tile([P, HALF], F32, name=f"result0_{n}")
+            nc.vector.tensor_tensor(result[:], residual_rows[n][:].indirect(half_list(0)), product[:], ADD)
+            store(0, n, result)
+
         v_mx = [gather_states(0)]
-        wg_mx = [reorder_gate_weight(0)]
+        wg_mx = [reorder_gate_weight(a) for a in range(R_BLOCKS)]
         wu_mx = [quantize_up_weight(0)]
+        v_mx.append(gather_states(1))
+
+        h_mx = ([], [])
         picked = []
-        for h in range(2):
-            sums = [psum.tile([P, HALF], F32, name=f"down_bank{n}") for n in range(N_TILES)]
-            for a in range(R_BLOCKS):
-                gated = gate(a, wg_mx[a], v_mx[h])
-                if h == 0 and a + 1 < R_BLOCKS:
-                    wg_mx.append(reorder_gate_weight(a + 1))
-                    wu_mx.append(quantize_up_weight(a + 1))
-                down(a, up_and_product(gated, wu_mx[a], v_mx[h]), sums)
-                if h == 0 and a == 0:
-                    v_mx.append(gather_states(1))
-            if h == 0:
-                for n in range(N_TILES):
-                    product = keep.tile([P, HALF], F32, name=f"product{n}")
-                    nc.scalar.copy(out=product[:], in_=sums[n][:])
-                    g_picked = keep.tile([P, HALF], F32, name=f"picked{n}")
-                    nc.vector.tensor_copy(g_picked[:], residual_rows[n][:].indirect(half_list(1)))
-                    picked.append((product, g_picked))
-            else:
-                for n in range(N_TILES):
-                    result = keep.tile([P, HALF], F32, name=f"result0_{n}")
-                    nc.vector.tensor_tensor(
-                        result[:], residual_rows[n][:].indirect(half_list(0)), picked[n][0][:], ADD
-                    )
-                    store(0, n, result)
-                for n in range(N_TILES):
-                    result = keep.tile([P, HALF], F32, name=f"result1_{n}")
-                    nc.vector.tensor_tensor(out=result[:], in0=sums[n][:], in1=picked[n][1][:], op=ADD)
-                    store(1, n, result)
+        for a in range(R_BLOCKS):
+            gated = [gate(a, wg_mx[a], v_mx[h]) for h in range(2)]
+            if a + 1 < R_BLOCKS:
+                wu_mx.append(quantize_up_weight(a + 1))
+            h_mx[0].append(up_and_product(gated[0], wu_mx[a], v_mx[0]))
+            if a > 0:
+                picked.extend(pick_residual(n) for n in (2 * a - 2, 2 * a - 1))
+            h_mx[1].append(up_and_product(gated[1], wu_mx[a], v_mx[1]))
+        for n in range(N_TILES):
+            finish_first_half(n)
+        for n in range(N_TILES):
+            result = keep.tile([P, HALF], F32, name=f"result1_{n}")
+            nc.vector.tensor_tensor(out=result[:], in0=down(n, h_mx[1])[:], in1=picked[n][:], op=ADD)
+            store(1, n, result)

@@ -41,6 +41,8 @@ def tile_list_paged_swiglu_residual_kernel(
         work = ctx.enter_context(tc.tile_pool(name="work", bufs=2))
         psum = ctx.enter_context(tc.psum_pool(name="psum", bufs=1))
 
+        wg_raw = keep.tile([P, H // 2], I32, name="wg_raw", align_bytes=64)
+        nc.sync.dma_start(out=wg_raw[:], in_=wg_words[0].bitcast(I32))
         offsets = keep.tile([P, S // 16], U16, name="offsets")
         nc.sync.dma_start(offsets[:], offs)
 
@@ -51,14 +53,12 @@ def tile_list_paged_swiglu_residual_kernel(
         wd_plane = keep.tile([P, R_BLOCKS, N // 4], I32, name="wd_plane", align_bytes=64)
         nc.vector.memset(wd_plane[:], 0)
 
-        bias = keep.tile([P, R_BLOCKS, PACK], F32, name="bias")
-        nc.sync.dma_start(out=bias[:], in_=bg.rearrange("(a p t) -> p a t", p=P, t=PACK))
         load_scale_rows(nc.sync, tab_plane, tab_scales[0].bitcast(I32))
         tab_codes = keep.tile([P, T], I32, name="tab_codes", align_bytes=64)
         nc.sync.dma_start(out=tab_codes[:], in_=tab_words[0].rearrange("p t i -> p (t i)").bitcast(I32))
-        wg_raw = keep.tile([P, H // 2], I32, name="wg_raw", align_bytes=64)
-        nc.sync.dma_start(out=wg_raw[:], in_=wg_words[0].bitcast(I32))
         load_scale_rows(nc.sync, wg_plane_raw, wg_scales[0].bitcast(I32))
+        bias = keep.tile([P, R_BLOCKS, PACK], F32, name="bias")
+        nc.sync.dma_start(out=bias[:], in_=bg.rearrange("(a p t) -> p a t", p=P, t=PACK))
 
         def load_up_weight(a):
             raw = keep.tile([P, PACK * PASS], F32, name=f"wu_raw{a}")
@@ -73,13 +73,11 @@ def tile_list_paged_swiglu_residual_kernel(
             nc.sync.dma_start(out=g_rows[:], in_=gT[n * P : (n + 1) * P, :])
             return g_rows
 
-        wu_raw = [load_up_weight(0), load_up_weight(1)]
-        residual_rows = [load_residual_rows(0)]
-        wu_raw.append(load_up_weight(2))
-        residual_rows.extend(load_residual_rows(n) for n in range(1, N_TILES))
+        wu_raw = [load_up_weight(a) for a in range(R_BLOCKS)]
         load_scale_rows(nc.sync, wd_plane, wd_scales.bitcast(I32).rearrange("a q c -> q a c"))
         wd_codes = keep.tile([P, R_BLOCKS, N], I32, name="wd_codes", align_bytes=64)
         nc.sync.dma_start(out=wd_codes[:], in_=wd_words.rearrange("a p c i -> p a (c i)").bitcast(I32))
+        residual_rows = [load_residual_rows(n) for n in range(N_TILES)]
 
         def half_list(h):
             cols = HALF // 16
@@ -180,17 +178,12 @@ def tile_list_paged_swiglu_residual_kernel(
         def store(h, n, result):
             nc.sync.dma_start(out=out[n * P : (n + 1) * P, h * HALF : (h + 1) * HALF], in_=result[:])
 
-        def pick_residual(n):
-            g_picked = keep.tile([P, HALF], F32, name=f"picked{n}")
-            nc.vector.tensor_copy(g_picked[:], residual_rows[n][:].indirect(half_list(1)))
-            return g_picked
-
-        def finish_first_half(n):
-            product = keep.tile([P, HALF], F32, name=f"product{n}")
-            nc.scalar.copy(out=product[:], in_=down(n, h_mx[0])[:])
-            result = keep.tile([P, HALF], F32, name=f"result0_{n}")
-            nc.vector.tensor_tensor(result[:], residual_rows[n][:].indirect(half_list(0)), product[:], ADD)
-            store(0, n, result)
+        def finish(h, n):
+            product = keep.tile([P, HALF], F32, name=f"product{h}_{n}")
+            nc.scalar.copy(out=product[:], in_=down(n, h_mx[h])[:])
+            result = keep.tile([P, HALF], F32, name=f"result{h}_{n}")
+            nc.vector.tensor_tensor(result[:], residual_rows[n][:].indirect(half_list(h)), product[:], ADD)
+            store(h, n, result)
 
         v_mx = [gather_states(0)]
         wg_mx = [reorder_gate_weight(a) for a in range(R_BLOCKS)]
@@ -198,18 +191,12 @@ def tile_list_paged_swiglu_residual_kernel(
         v_mx.append(gather_states(1))
 
         h_mx = ([], [])
-        picked = []
         for a in range(R_BLOCKS):
             gated = [gate(a, wg_mx[a], v_mx[h]) for h in range(2)]
             if a + 1 < R_BLOCKS:
                 wu_mx.append(quantize_up_weight(a + 1))
-            h_mx[0].append(up_and_product(gated[0], wu_mx[a], v_mx[0]))
-            if a > 0:
-                picked.extend(pick_residual(n) for n in (2 * a - 2, 2 * a - 1))
-            h_mx[1].append(up_and_product(gated[1], wu_mx[a], v_mx[1]))
-        for n in range(N_TILES):
-            finish_first_half(n)
-        for n in range(N_TILES):
-            result = keep.tile([P, HALF], F32, name=f"result1_{n}")
-            nc.vector.tensor_tensor(out=result[:], in0=down(n, h_mx[1])[:], in1=picked[n][:], op=ADD)
-            store(1, n, result)
+            for h in range(2):
+                h_mx[h].append(up_and_product(gated[h], wu_mx[a], v_mx[h]))
+        for h in range(2):
+            for n in range(N_TILES):
+                finish(h, n)

@@ -25,11 +25,13 @@ N_TILES = N // P
 HALF = S // 2
 CHUNK = 128
 RUN = 2
+SCALAR_ROWS = (64, 128, 104)
+LAST_PIECE = 128
 
 
 def load_scale_rows(queue, plane, rows):
-    for q in range(4):
-        queue.dma_start(out=plane[32 * q : 32 * q + 4], in_=rows[4 * q : 4 * q + 4])
+    for r in range(4):
+        queue.dma_start(out=plane[r:P:32], in_=rows[r:16:4])
 
 
 def tile_list_paged_swiglu_residual_kernel(
@@ -49,22 +51,24 @@ def tile_list_paged_swiglu_residual_kernel(
         tab_plane = keep.tile([P, T // 4], I32, name="tab_plane", align_bytes=64)
         nc.vector.memset(tab_plane[:], 0)
         wg_plane_raw = keep.tile([P, H // 4], I32, name="wg_plane_raw", tag="wg_plane_raw", align_bytes=64)
-        nc.vector.memset(wg_plane_raw[:], 0)
+        nc.gpsimd.memset(wg_plane_raw[:], 0)
         wd_plane = keep.tile([P, R_BLOCKS, N // 4], I32, name="wd_plane", align_bytes=64)
-        nc.vector.memset(wd_plane[:], 0)
+        nc.gpsimd.memset(wd_plane[:], 0)
+        warm = keep.tile([P, 2], F32, name="warm")
+        nc.gpsimd.memset(warm[:, 0:1], 0.0)
+        nc.scalar.activation(out=warm[:, 1:2], in_=warm[:, 0:1], func=SILU)
 
         load_scale_rows(nc.sync, tab_plane, tab_scales[0].bitcast(I32))
         tab_codes = keep.tile([P, T], I32, name="tab_codes", align_bytes=64)
         nc.sync.dma_start(out=tab_codes[:], in_=tab_words[0].rearrange("p t i -> p (t i)").bitcast(I32))
-        load_scale_rows(nc.sync, wg_plane_raw, wg_scales[0].bitcast(I32))
         bias = keep.tile([P, R_BLOCKS, PACK], F32, name="bias")
         nc.sync.dma_start(out=bias[:], in_=bg.rearrange("(a p t) -> p a t", p=P, t=PACK))
 
-        def load_up_weight(a):
-            raw = keep.tile([P, PACK * PASS], F32, name=f"wu_raw{a}")
+        def load_up_weight(first, width):
+            raw = keep.tile([P, PACK * width], F32, name=f"wu_raw{first}")
             nc.sync.dma_start(
                 out=raw[:].rearrange("p (j c) -> p j c", j=PACK),
-                in_=wu[:, a * PASS : (a + 1) * PASS].rearrange("(p j) c -> p j c", j=PACK),
+                in_=wu[:, first : first + width].rearrange("(p j) c -> p j c", j=PACK),
             )
             return raw
 
@@ -73,7 +77,10 @@ def tile_list_paged_swiglu_residual_kernel(
             nc.sync.dma_start(out=g_rows[:], in_=gT[n * P : (n + 1) * P, :])
             return g_rows
 
-        wu_raw = [load_up_weight(a) for a in range(R_BLOCKS)]
+        first_part = load_up_weight(0, PASS // 2)
+        load_scale_rows(nc.sync, wg_plane_raw, wg_scales[0].bitcast(I32))
+        wu_raw = [[first_part, load_up_weight(PASS // 2, PASS // 2)]]
+        wu_raw.extend([load_up_weight(a * PASS, PASS)] for a in range(1, R_BLOCKS))
         load_scale_rows(nc.sync, wd_plane, wd_scales.bitcast(I32).rearrange("a q c -> q a c"))
         wd_codes = keep.tile([P, R_BLOCKS, N], I32, name="wd_codes", align_bytes=64)
         nc.sync.dma_start(out=wd_codes[:], in_=wd_words.rearrange("a p c i -> p a (c i)").bitcast(I32))
@@ -87,7 +94,13 @@ def tile_list_paged_swiglu_residual_kernel(
             plane = keep.tile([P, HALF], U8, name=f"v_plane{h}", align_bytes=64)
             nc.vector.tensor_copy(plane[:], tab_plane[:].bitcast(U8).indirect(half_list(h)))
             codes = keep.tile([P, HALF], U32, name=f"v_codes{h}", tag=("v_codes0", "wg_plane_raw")[h], align_bytes=64)
-            nc.vector.tensor_copy(codes[:], tab_codes[:].bitcast(U32).indirect(half_list(h)))
+            pieces = 2 if h == 0 else 1
+            width = HALF // pieces
+            for e in range(pieces):
+                cols = slice(e * width // 16, (e + 1) * width // 16)
+                nc.vector.tensor_copy(
+                    codes[:, e * width : (e + 1) * width], tab_codes[:].bitcast(U32).indirect(half_list(h)[:, cols])
+                )
             return codes, plane
 
         def reorder_gate_weight(a):
@@ -107,30 +120,37 @@ def tile_list_paged_swiglu_residual_kernel(
         def quantize_up_weight(a):
             grouped = work.tile([P, PASS * PACK], BF16, name="wu_grouped", align_bytes=64)
             dst = grouped[:].rearrange("p (t m j) -> p m j t", t=PACK, j=PACK)
-            src = wu_raw[a][:].rearrange("p (j m t) -> p m j t", j=PACK, t=PACK)
+            src = [raw[:].rearrange("p (j m t) -> p m j t", j=PACK, t=PACK) for raw in wu_raw[a]]
+            rows = SCALAR_ROWS[a]
+            nc.scalar.copy(out=dst[:, :rows], in_=src[0][:, :rows])
             if a == 0:
-                nc.vector.tensor_copy(out=dst, in_=src)
-            else:
-                nc.scalar.copy(out=dst, in_=src)
+                nc.vector.tensor_copy(out=dst[:, rows:], in_=src[1])
+            elif rows < P:
+                nc.vector.tensor_copy(out=dst[:, rows:], in_=src[0][:, rows:])
             codes = keep.tile([P, PASS], U32, name=f"wu_codes{a}", align_bytes=64)
             plane = keep.tile([P, PASS], U8, name=f"wu_plane{a}", align_bytes=64)
             nc.vector.quantize_mx(out=codes[:].bitcast(FP8X4), scales=plane[:], in_=grouped[:])
             return codes, plane
 
-        def gate(a, wg_mx, v_mx):
+        def gate(a, wg_mx, v_mx, pieces):
             gated = work.tile([P, PACK, HALF], F32, name="gated", bufs=3)
-            for t in range(PACK):
-                bank = psum.tile([P, HALF], F32, name="wide_bank", bufs=4)
-                nc.tensor.matmul_mx(
-                    out=bank[:],
-                    lhsT=wg_mx[0][:].bitcast(U8)[:, 2 * P * t : 2 * P * (t + 1)].bitcast(FP4X4),
-                    lhsT_scale=wg_mx[1][:, P * t : P * (t + 1)],
-                    rhs=v_mx[0][:].bitcast(FP8X4),
-                    rhs_scale=v_mx[1][:],
-                    start=True,
-                    stop=True,
-                )
-                nc.scalar.activation(out=gated[:, t, :], in_=bank[:], func=SILU, bias=bias[:, a, t : t + 1])
+            width = HALF // pieces
+            for e in range(pieces):
+                tokens = slice(e * width, (e + 1) * width)
+                for t in range(PACK):
+                    bank = psum.tile([P, HALF], F32, name="wide_bank", bufs=4)
+                    nc.tensor.matmul_mx(
+                        out=bank[:, :width],
+                        lhsT=wg_mx[0][:].bitcast(U8)[:, 2 * P * t : 2 * P * (t + 1)].bitcast(FP4X4),
+                        lhsT_scale=wg_mx[1][:, P * t : P * (t + 1)],
+                        rhs=v_mx[0][:, tokens].bitcast(FP8X4),
+                        rhs_scale=v_mx[1][:, tokens],
+                        start=True,
+                        stop=True,
+                    )
+                    nc.scalar.activation(
+                        out=gated[:, t, tokens], in_=bank[:, :width], func=SILU, bias=bias[:, a, t : t + 1]
+                    )
             return gated
 
         def up_and_product(gated, wu_mx, v_mx):
@@ -175,15 +195,17 @@ def tile_list_paged_swiglu_residual_kernel(
                 )
             return bank
 
-        def store(h, n, result):
-            nc.sync.dma_start(out=out[n * P : (n + 1) * P, h * HALF : (h + 1) * HALF], in_=result[:])
-
         def finish(h, n):
             product = keep.tile([P, HALF], F32, name=f"product{h}_{n}")
             nc.scalar.copy(out=product[:], in_=down(n, h_mx[h])[:])
             result = keep.tile([P, HALF], F32, name=f"result{h}_{n}")
-            nc.vector.tensor_tensor(result[:], residual_rows[n][:].indirect(half_list(h)), product[:], ADD)
-            store(h, n, result)
+            cuts = (0, HALF - LAST_PIECE, HALF) if (h, n) == (1, N_TILES - 1) else (0, HALF)
+            for first, end in zip(cuts, cuts[1:]):
+                picked = residual_rows[n][:].indirect(half_list(h)[:, first // 16 : end // 16])
+                nc.vector.tensor_tensor(result[:, first:end], picked, product[:, first:end], ADD)
+                nc.sync.dma_start(
+                    out=out[n * P : (n + 1) * P, h * HALF + first : h * HALF + end], in_=result[:, first:end]
+                )
 
         v_mx = [gather_states(0)]
         wg_mx = [reorder_gate_weight(a) for a in range(R_BLOCKS)]
@@ -192,7 +214,7 @@ def tile_list_paged_swiglu_residual_kernel(
 
         h_mx = ([], [])
         for a in range(R_BLOCKS):
-            gated = [gate(a, wg_mx[a], v_mx[h]) for h in range(2)]
+            gated = [gate(a, wg_mx[a], v_mx[h], 2 if a + h == 0 else 1) for h in range(2)]
             if a + 1 < R_BLOCKS:
                 wu_mx.append(quantize_up_weight(a + 1))
             for h in range(2):

@@ -25,7 +25,7 @@ N_TILES = N // P
 HALF = S // 2
 CHUNK = 128
 RUN = 2
-SCALAR_ROWS = (64, 128, 104)
+SCALAR_ROWS = (64, 80, 112)
 LAST_PIECE = 128
 
 
@@ -51,11 +51,11 @@ def tile_list_paged_swiglu_residual_kernel(
         tab_plane = keep.tile([P, T // 4], I32, name="tab_plane", align_bytes=64)
         nc.vector.memset(tab_plane[:], 0)
         wg_plane_raw = keep.tile([P, H // 4], I32, name="wg_plane_raw", tag="wg_plane_raw", align_bytes=64)
-        nc.gpsimd.memset(wg_plane_raw[:], 0)
+        nc.vector.memset(wg_plane_raw[:], 0)
         wd_plane = keep.tile([P, R_BLOCKS, N // 4], I32, name="wd_plane", align_bytes=64)
-        nc.gpsimd.memset(wd_plane[:], 0)
+        nc.vector.memset(wd_plane[:], 0)
         warm = keep.tile([P, 2], F32, name="warm")
-        nc.gpsimd.memset(warm[:, 0:1], 0.0)
+        nc.vector.memset(warm[:, 0:1], 0.0)
         nc.scalar.activation(out=warm[:, 1:2], in_=warm[:, 0:1], func=SILU)
 
         load_scale_rows(nc.sync, tab_plane, tab_scales[0].bitcast(I32))
@@ -80,7 +80,10 @@ def tile_list_paged_swiglu_residual_kernel(
         first_part = load_up_weight(0, PASS // 2)
         load_scale_rows(nc.sync, wg_plane_raw, wg_scales[0].bitcast(I32))
         wu_raw = [[first_part, load_up_weight(PASS // 2, PASS // 2)]]
-        wu_raw.extend([load_up_weight(a * PASS, PASS)] for a in range(1, R_BLOCKS))
+        cut = PACK * SCALAR_ROWS[1]
+        vector_part = load_up_weight(PASS + cut, PASS - cut)
+        wu_raw.append([load_up_weight(PASS, cut), vector_part])
+        wu_raw.append([load_up_weight(2 * PASS, PASS)])
         load_scale_rows(nc.sync, wd_plane, wd_scales.bitcast(I32).rearrange("a q c -> q a c"))
         wd_codes = keep.tile([P, R_BLOCKS, N], I32, name="wd_codes", align_bytes=64)
         nc.sync.dma_start(out=wd_codes[:], in_=wd_words.rearrange("a p c i -> p a (c i)").bitcast(I32))
@@ -90,9 +93,11 @@ def tile_list_paged_swiglu_residual_kernel(
             cols = HALF // 16
             return offsets[:, h * cols : (h + 1) * cols]
 
+        v_plane = keep.tile([P, S], U8, name="v_plane", align_bytes=64)
+        nc.vector.tensor_copy(v_plane[:], tab_plane[:].bitcast(U8).indirect(offsets[:]))
+
         def gather_states(h):
-            plane = keep.tile([P, HALF], U8, name=f"v_plane{h}", align_bytes=64)
-            nc.vector.tensor_copy(plane[:], tab_plane[:].bitcast(U8).indirect(half_list(h)))
+            plane = v_plane[:, h * HALF : (h + 1) * HALF]
             codes = keep.tile([P, HALF], U32, name=f"v_codes{h}", tag=("v_codes0", "wg_plane_raw")[h], align_bytes=64)
             pieces = 2 if h == 0 else 1
             width = HALF // pieces
@@ -103,27 +108,26 @@ def tile_list_paged_swiglu_residual_kernel(
                 )
             return codes, plane
 
-        def reorder_gate_weight(a):
-            cols = slice(a * PASS, (a + 1) * PASS)
-            codes = keep.tile([P, PASS], U16, name=f"wg_codes{a}", align_bytes=64)
-            nc.vector.tensor_copy(
-                out=codes[:].rearrange("p (t m) -> p t m", t=PACK),
-                in_=wg_raw[:].bitcast(U16)[:, cols].rearrange("p (m t) -> p t m", t=PACK),
-            )
-            plane = keep.tile([P, PASS], U8, name=f"wg_plane{a}", align_bytes=64)
-            nc.vector.tensor_copy(
-                out=plane[:].rearrange("p (t m) -> p t m", t=PACK),
-                in_=wg_plane_raw[:].bitcast(U8)[:, cols].rearrange("p (m t) -> p t m", t=PACK),
-            )
-            return codes, plane
+        def reorder_gate(name, raw, dtype):
+            blocks = []
+            for first, count in ((0, 1), (1, R_BLOCKS - 1)):
+                ordered = keep.tile([P, count * PASS], dtype, name=f"{name}{first}", align_bytes=64)
+                nc.vector.tensor_copy(
+                    out=ordered[:].rearrange("p (a t m) -> p a t m", t=PACK, m=P),
+                    in_=raw[:]
+                    .bitcast(dtype)[:, first * PASS : (first + count) * PASS]
+                    .rearrange("p (a m t) -> p a t m", t=PACK, m=P),
+                )
+                blocks.extend(ordered[:, a * PASS : (a + 1) * PASS] for a in range(count))
+            return blocks
 
         def quantize_up_weight(a):
-            grouped = work.tile([P, PASS * PACK], BF16, name="wu_grouped", align_bytes=64)
+            grouped = work.tile([P, PASS * PACK], BF16, name="wu_grouped", bufs=1, align_bytes=64)
             dst = grouped[:].rearrange("p (t m j) -> p m j t", t=PACK, j=PACK)
             src = [raw[:].rearrange("p (j m t) -> p m j t", j=PACK, t=PACK) for raw in wu_raw[a]]
             rows = SCALAR_ROWS[a]
             nc.scalar.copy(out=dst[:, :rows], in_=src[0][:, :rows])
-            if a == 0:
+            if a < 2:
                 nc.vector.tensor_copy(out=dst[:, rows:], in_=src[1])
             elif rows < P:
                 nc.vector.tensor_copy(out=dst[:, rows:], in_=src[0][:, rows:])
@@ -141,7 +145,7 @@ def tile_list_paged_swiglu_residual_kernel(
                     bank = psum.tile([P, HALF], F32, name="wide_bank", bufs=4)
                     nc.tensor.matmul_mx(
                         out=bank[:, :width],
-                        lhsT=wg_mx[0][:].bitcast(U8)[:, 2 * P * t : 2 * P * (t + 1)].bitcast(FP4X4),
+                        lhsT=wg_mx[0].bitcast(U8)[:, 2 * P * t : 2 * P * (t + 1)].bitcast(FP4X4),
                         lhsT_scale=wg_mx[1][:, P * t : P * (t + 1)],
                         rhs=v_mx[0][:, tokens].bitcast(FP8X4),
                         rhs_scale=v_mx[1][:, tokens],
@@ -208,7 +212,7 @@ def tile_list_paged_swiglu_residual_kernel(
                 )
 
         v_mx = [gather_states(0)]
-        wg_mx = [reorder_gate_weight(a) for a in range(R_BLOCKS)]
+        wg_mx = list(zip(reorder_gate("wg_codes", wg_raw, U16), reorder_gate("wg_plane", wg_plane_raw, U8)))
         wu_mx = [quantize_up_weight(0)]
         v_mx.append(gather_states(1))
 

@@ -25,13 +25,13 @@ N_TILES = N // P
 HALF = S // 2
 CHUNK = 128
 RUN = 2
-SCALAR_ROWS = (64, 80, 112)
+SCALAR_ROWS = (64, 128, 104)
 LAST_PIECE = 128
 
 
 def load_scale_rows(queue, plane, rows):
-    for r in range(4):
-        queue.dma_start(out=plane[r:P:32], in_=rows[r:16:4])
+    for q in range(4):
+        queue.dma_start(out=plane[32 * q : 32 * q + 4], in_=rows[4 * q : 4 * q + 4])
 
 
 def tile_list_paged_swiglu_residual_kernel(
@@ -50,8 +50,10 @@ def tile_list_paged_swiglu_residual_kernel(
 
         tab_plane = keep.tile([P, T // 4], I32, name="tab_plane", align_bytes=64)
         nc.vector.memset(tab_plane[:], 0)
-        wg_plane_raw = keep.tile([P, H // 4], I32, name="wg_plane_raw", tag="wg_plane_raw", align_bytes=64)
-        nc.vector.memset(wg_plane_raw[:], 0)
+        wg_plane_first = keep.tile([P, PASS // 4], I32, name="wg_plane_first", tag="wg_plane_first", align_bytes=64)
+        nc.vector.memset(wg_plane_first[:], 0)
+        wg_plane_rest = keep.tile([P, (H - PASS) // 4], I32, name="wg_plane_rest", align_bytes=64)
+        nc.vector.memset(wg_plane_rest[:], 0)
         wd_plane = keep.tile([P, R_BLOCKS, N // 4], I32, name="wd_plane", align_bytes=64)
         nc.vector.memset(wd_plane[:], 0)
         warm = keep.tile([P, 2], F32, name="warm")
@@ -61,11 +63,12 @@ def tile_list_paged_swiglu_residual_kernel(
         load_scale_rows(nc.sync, tab_plane, tab_scales[0].bitcast(I32))
         tab_codes = keep.tile([P, T], I32, name="tab_codes", align_bytes=64)
         nc.sync.dma_start(out=tab_codes[:], in_=tab_words[0].rearrange("p t i -> p (t i)").bitcast(I32))
+        load_scale_rows(nc.sync, wg_plane_first, wg_scales[0].bitcast(I32)[:, : PASS // 4])
         bias = keep.tile([P, R_BLOCKS, PACK], F32, name="bias")
         nc.sync.dma_start(out=bias[:], in_=bg.rearrange("(a p t) -> p a t", p=P, t=PACK))
 
         def load_up_weight(first, width):
-            raw = keep.tile([P, PACK * width], F32, name=f"wu_raw{first}")
+            raw = keep.tile([P, PACK * width], F32, name=f"wu_raw{first}", tag=f"wu_raw{first}", align_bytes=64)
             nc.sync.dma_start(
                 out=raw[:].rearrange("p (j c) -> p j c", j=PACK),
                 in_=wu[:, first : first + width].rearrange("(p j) c -> p j c", j=PACK),
@@ -77,12 +80,9 @@ def tile_list_paged_swiglu_residual_kernel(
             nc.sync.dma_start(out=g_rows[:], in_=gT[n * P : (n + 1) * P, :])
             return g_rows
 
-        first_part = load_up_weight(0, PASS // 2)
-        load_scale_rows(nc.sync, wg_plane_raw, wg_scales[0].bitcast(I32))
-        wu_raw = [[first_part, load_up_weight(PASS // 2, PASS // 2)]]
-        cut = PACK * SCALAR_ROWS[1]
-        vector_part = load_up_weight(PASS + cut, PASS - cut)
-        wu_raw.append([load_up_weight(PASS, cut), vector_part])
+        wu_raw = [[load_up_weight(0, PASS // 2), load_up_weight(PASS // 2, PASS // 2)]]
+        load_scale_rows(nc.sync, wg_plane_rest, wg_scales[0].bitcast(I32)[:, PASS // 4 :])
+        wu_raw.append([load_up_weight(PASS, PASS)])
         wu_raw.append([load_up_weight(2 * PASS, PASS)])
         load_scale_rows(nc.sync, wd_plane, wd_scales.bitcast(I32).rearrange("a q c -> q a c"))
         wd_codes = keep.tile([P, R_BLOCKS, N], I32, name="wd_codes", align_bytes=64)
@@ -98,8 +98,8 @@ def tile_list_paged_swiglu_residual_kernel(
 
         def gather_states(h):
             plane = v_plane[:, h * HALF : (h + 1) * HALF]
-            codes = keep.tile([P, HALF], U32, name=f"v_codes{h}", tag=("v_codes0", "wg_plane_raw")[h], align_bytes=64)
-            pieces = 2 if h == 0 else 1
+            codes = keep.tile([P, HALF], U32, name=f"v_codes{h}", tag=("v_codes0", "wg_plane_first")[h], align_bytes=64)
+            pieces = 1
             width = HALF // pieces
             for e in range(pieces):
                 cols = slice(e * width // 16, (e + 1) * width // 16)
@@ -108,36 +108,42 @@ def tile_list_paged_swiglu_residual_kernel(
                 )
             return codes, plane
 
-        def reorder_gate(name, raw, dtype):
-            blocks = []
-            for first, count in ((0, 1), (1, R_BLOCKS - 1)):
-                ordered = keep.tile([P, count * PASS], dtype, name=f"{name}{first}", align_bytes=64)
-                nc.vector.tensor_copy(
-                    out=ordered[:].rearrange("p (a t m) -> p a t m", t=PACK, m=P),
-                    in_=raw[:]
-                    .bitcast(dtype)[:, first * PASS : (first + count) * PASS]
-                    .rearrange("p (a m t) -> p a t m", t=PACK, m=P),
-                )
-                blocks.extend(ordered[:, a * PASS : (a + 1) * PASS] for a in range(count))
-            return blocks
+        def reorder(engine, ordered, raw):
+            engine.tensor_copy(
+                out=ordered.rearrange("p (a t m) -> p a t m", t=PACK, m=P),
+                in_=raw.rearrange("p (a m t) -> p a t m", t=PACK, m=P),
+            )
 
-        def quantize_up_weight(a):
-            grouped = work.tile([P, PASS * PACK], BF16, name="wu_grouped", bufs=1, align_bytes=64)
+        def round_up_weight(a):
+            grouped = keep.tile([P, PASS * PACK], BF16, name=f"wu_grouped{a}", tag=f"wu_grouped{a}", align_bytes=64)
             dst = grouped[:].rearrange("p (t m j) -> p m j t", t=PACK, j=PACK)
             src = [raw[:].rearrange("p (j m t) -> p m j t", j=PACK, t=PACK) for raw in wu_raw[a]]
             rows = SCALAR_ROWS[a]
-            nc.scalar.copy(out=dst[:, :rows], in_=src[0][:, :rows])
-            if a < 2:
-                nc.vector.tensor_copy(out=dst[:, rows:], in_=src[1])
-            elif rows < P:
-                nc.vector.tensor_copy(out=dst[:, rows:], in_=src[0][:, rows:])
+            if rows > 0:
+                nc.scalar.copy(out=dst[:, :rows], in_=src[0][:, :rows])
+            if rows < P:
+                nc.vector.tensor_copy(out=dst[:, rows:], in_=src[1] if a == 0 else src[0][:, rows:])
+            return grouped
+
+        def quantize_up_weight(a, grouped):
             codes = keep.tile([P, PASS], U32, name=f"wu_codes{a}", align_bytes=64)
             plane = keep.tile([P, PASS], U8, name=f"wu_plane{a}", align_bytes=64)
-            nc.vector.quantize_mx(out=codes[:].bitcast(FP8X4), scales=plane[:], in_=grouped[:])
+            pieces = PACK if a == 0 else 1
+            width = PASS // pieces
+            for e in range(pieces):
+                cols = slice(e * width, (e + 1) * width)
+                nc.vector.quantize_mx(
+                    out=codes[:, cols].bitcast(FP8X4),
+                    scales=plane[:, cols],
+                    in_=grouped[:, PACK * e * width : PACK * (e + 1) * width],
+                )
             return codes, plane
 
-        def gate(a, wg_mx, v_mx, pieces):
-            gated = work.tile([P, PACK, HALF], F32, name="gated", bufs=3)
+        def gate(a, h, wg_mx, v_mx, pieces):
+            if a + h == 0:
+                gated = keep.tile([P, PACK, HALF], F32, name=f"gated{a}", tag=f"wu_raw{a * PASS}", align_bytes=64)
+            else:
+                gated = work.tile([P, PACK, HALF], F32, name="gated", bufs=3)
             width = HALF // pieces
             for e in range(pieces):
                 tokens = slice(e * width, (e + 1) * width)
@@ -212,17 +218,26 @@ def tile_list_paged_swiglu_residual_kernel(
                 )
 
         v_mx = [gather_states(0)]
-        wg_mx = list(zip(reorder_gate("wg_codes", wg_raw, U16), reorder_gate("wg_plane", wg_plane_raw, U8)))
-        wu_mx = [quantize_up_weight(0)]
+        wg_codes = keep.tile([P, H], U16, name="wg_codes", align_bytes=64)
+        reorder(nc.vector, wg_codes[:, :PASS], wg_raw[:].bitcast(U16)[:, :PASS])
+        reorder(nc.vector, wg_codes[:, PASS:], wg_raw[:].bitcast(U16)[:, PASS:])
+        first_plane = keep.tile([P, PASS], U8, name="first_plane", align_bytes=64)
+        reorder(nc.vector, first_plane[:], wg_plane_first[:].bitcast(U8))
+        wu_mx = [quantize_up_weight(0, round_up_weight(0))]
         v_mx.append(gather_states(1))
 
         h_mx = ([], [])
+        later = keep.tile([P, H - PASS], U8, name="later_planes", tag="wu_grouped0", align_bytes=64)
+        reorder(nc.vector, later[:], wg_plane_rest[:].bitcast(U8))
+        planes = [first_plane[:], later[:, :PASS], later[:, PASS:]]
         for a in range(R_BLOCKS):
-            gated = [gate(a, wg_mx[a], v_mx[h], 2 if a + h == 0 else 1) for h in range(2)]
+            gated = [gate(a, h, (wg_codes[:, a * PASS : (a + 1) * PASS], planes[a]), v_mx[h], 1) for h in range(2)]
             if a + 1 < R_BLOCKS:
-                wu_mx.append(quantize_up_weight(a + 1))
+                grouped = round_up_weight(a + 1)
             for h in range(2):
                 h_mx[h].append(up_and_product(gated[h], wu_mx[a], v_mx[h]))
+                if h == 0 and a + 1 < R_BLOCKS:
+                    wu_mx.append(quantize_up_weight(a + 1, grouped))
         for h in range(2):
             for n in range(N_TILES):
                 finish(h, n)

@@ -25,8 +25,17 @@ N_TILES = N // P
 HALF = S // 2
 CHUNK = 128
 RUN = 2
-SCALAR_ROWS = (64, 128, 104)
 LAST_PIECE = 128
+PLACE = {
+    "wg_raw": 0,
+    "wg_plane1": 0,
+    "wu_grouped1": 512,
+    "hidden0_0": 4608,
+    "wu_grouped3": 4608,
+    "hidden0_1": 8704,
+    "wu_grouped2": 8704,
+    "wg_plane2": 11776,
+}
 
 
 def load_scale_rows(queue, plane, rows):
@@ -40,10 +49,16 @@ def tile_list_paged_swiglu_residual_kernel(
     nc = tc.nc
     with ExitStack() as ctx:
         keep = ctx.enter_context(tc.tile_pool(name="keep", bufs=1))
+        shared = ctx.enter_context(tc.tile_pool(name="shared", bufs=1))
         work = ctx.enter_context(tc.tile_pool(name="work", bufs=2))
         psum = ctx.enter_context(tc.psum_pool(name="psum", bufs=1))
 
-        wg_raw = keep.tile([P, H // 2], I32, name="wg_raw", align_bytes=64)
+        def placed(shape, dtype, name):
+            if name in PLACE:
+                return shared.tile(shape, dtype, name=name, align_bytes=64, offset=PLACE[name])
+            return keep.tile(shape, dtype, name=name, tag=name, align_bytes=64)
+
+        wg_raw = placed([P, H // 2], I32, "wg_raw")
         nc.sync.dma_start(out=wg_raw[:], in_=wg_words[0].bitcast(I32))
         offsets = keep.tile([P, S // 16], U16, name="offsets")
         nc.sync.dma_start(offsets[:], offs)
@@ -81,8 +96,8 @@ def tile_list_paged_swiglu_residual_kernel(
             return g_rows
 
         wu_raw = [[load_up_weight(0, PASS // 2), load_up_weight(PASS // 2, PASS // 2)]]
-        load_scale_rows(nc.sync, wg_plane_rest, wg_scales[0].bitcast(I32)[:, PASS // 4 :])
         wu_raw.append([load_up_weight(PASS, PASS)])
+        load_scale_rows(nc.sync, wg_plane_rest, wg_scales[0].bitcast(I32)[:, PASS // 4 :])
         wu_raw.append([load_up_weight(2 * PASS, PASS)])
         load_scale_rows(nc.sync, wd_plane, wd_scales.bitcast(I32).rearrange("a q c -> q a c"))
         wd_codes = keep.tile([P, R_BLOCKS, N], I32, name="wd_codes", align_bytes=64)
@@ -114,29 +129,29 @@ def tile_list_paged_swiglu_residual_kernel(
                 in_=raw.rearrange("p (a m t) -> p a t m", t=PACK, m=P),
             )
 
-        def round_up_weight(a):
-            grouped = keep.tile([P, PASS * PACK], BF16, name=f"wu_grouped{a}", tag=f"wu_grouped{a}", align_bytes=64)
-            dst = grouped[:].rearrange("p (t m j) -> p m j t", t=PACK, j=PACK)
-            src = [raw[:].rearrange("p (j m t) -> p m j t", j=PACK, t=PACK) for raw in wu_raw[a]]
-            rows = SCALAR_ROWS[a]
-            if rows > 0:
-                nc.scalar.copy(out=dst[:, :rows], in_=src[0][:, :rows])
-            if rows < P:
-                nc.vector.tensor_copy(out=dst[:, rows:], in_=src[1] if a == 0 else src[0][:, rows:])
-            return grouped
+        def grouped_tile(name, slots):
+            tile = placed([P, slots * P * PACK], BF16, name)
+            return tile, tile[:].rearrange("p (t m j) -> p m j t", t=slots, j=PACK)
 
-        def quantize_up_weight(a, grouped):
+        def reorder_plane(a):
+            plane = placed([P, PASS], U8, f"wg_plane{a}")
+            reorder(nc.gpsimd, plane[:], wg_plane_rest[:].bitcast(U8)[:, (a - 1) * PASS : a * PASS])
+            planes.append(plane[:])
+
+        def raw_view(raw):
+            return raw[:].rearrange("p (j m t) -> p m j t", j=PACK, t=PACK)
+
+        def round_on_gpsimd(dst, src):
+            nc.gpsimd.tensor_scalar(dst, src, 1.0, 0.0, MULT, ADD)
+
+        def quantize_up_weight(a, parts):
             codes = keep.tile([P, PASS], U32, name=f"wu_codes{a}", align_bytes=64)
             plane = keep.tile([P, PASS], U8, name=f"wu_plane{a}", align_bytes=64)
-            pieces = PACK if a == 0 else 1
-            width = PASS // pieces
-            for e in range(pieces):
-                cols = slice(e * width, (e + 1) * width)
-                nc.vector.quantize_mx(
-                    out=codes[:, cols].bitcast(FP8X4),
-                    scales=plane[:, cols],
-                    in_=grouped[:, PACK * e * width : PACK * (e + 1) * width],
-                )
+            first = 0
+            for part in parts:
+                end = first + part.shape[1] // PACK
+                nc.vector.quantize_mx(out=codes[:, first:end].bitcast(FP8X4), scales=plane[:, first:end], in_=part)
+                first = end
             return codes, plane
 
         def gate(a, h, wg_mx, v_mx, pieces):
@@ -163,8 +178,8 @@ def tile_list_paged_swiglu_residual_kernel(
                     )
             return gated
 
-        def up_and_product(gated, wu_mx, v_mx):
-            hidden = work.tile([P, HALF * PACK], BF16, name="hidden", align_bytes=64)
+        def up_and_product(name, gated, wu_mx, v_mx):
+            hidden = placed([P, HALF * PACK], BF16, name)
             for c in range(HALF // CHUNK):
                 tokens = slice(c * CHUNK, (c + 1) * CHUNK)
                 bank = psum.tile([P, PACK, CHUNK], F32, name="up_bank", bufs=4)
@@ -218,26 +233,50 @@ def tile_list_paged_swiglu_residual_kernel(
                 )
 
         v_mx = [gather_states(0)]
-        wg_codes = keep.tile([P, H], U16, name="wg_codes", align_bytes=64)
-        reorder(nc.vector, wg_codes[:, :PASS], wg_raw[:].bitcast(U16)[:, :PASS])
-        reorder(nc.vector, wg_codes[:, PASS:], wg_raw[:].bitcast(U16)[:, PASS:])
+        first_codes = keep.tile([P, PASS], U16, name="first_codes", align_bytes=64)
+        reorder(nc.vector, first_codes[:], wg_raw[:].bitcast(U16)[:, :PASS])
         first_plane = keep.tile([P, PASS], U8, name="first_plane", align_bytes=64)
         reorder(nc.vector, first_plane[:], wg_plane_first[:].bitcast(U8))
-        wu_mx = [quantize_up_weight(0, round_up_weight(0))]
+        grouped, dst = grouped_tile("wu_grouped0", PACK)
+        nc.scalar.copy(out=dst[:, : P // 2], in_=raw_view(wu_raw[0][0]))
+        nc.vector.tensor_copy(out=dst[:, P // 2 :], in_=raw_view(wu_raw[0][1]))
+        wu_mx = [quantize_up_weight(0, [grouped[:, t * PASS : (t + 1) * PASS] for t in range(PACK)])]
         v_mx.append(gather_states(1))
 
         h_mx = ([], [])
-        later = keep.tile([P, H - PASS], U8, name="later_planes", tag="wu_grouped0", align_bytes=64)
-        reorder(nc.vector, later[:], wg_plane_rest[:].bitcast(U8))
-        planes = [first_plane[:], later[:, :PASS], later[:, PASS:]]
-        for a in range(R_BLOCKS):
-            gated = [gate(a, h, (wg_codes[:, a * PASS : (a + 1) * PASS], planes[a]), v_mx[h], 1) for h in range(2)]
-            if a + 1 < R_BLOCKS:
-                grouped = round_up_weight(a + 1)
-            for h in range(2):
-                h_mx[h].append(up_and_product(gated[h], wu_mx[a], v_mx[h]))
-                if h == 0 and a + 1 < R_BLOCKS:
-                    wu_mx.append(quantize_up_weight(a + 1, grouped))
+        later = keep.tile([P, H - PASS], U16, name="later_codes", tag="wu_grouped0", align_bytes=64)
+        reorder(nc.vector, later[:], wg_raw[:].bitcast(U16)[:, PASS:])
+        codes = [first_codes[:], later[:, :PASS], later[:, PASS:]]
+        planes = [first_plane[:]]
+        src1, src2 = raw_view(wu_raw[1][0]), raw_view(wu_raw[2][0])
+
+        def gates(a):
+            return [gate(a, h, (codes[a], planes[a]), v_mx[h], 1) for h in range(2)]
+
+        def products(a, h):
+            h_mx[h].append(up_and_product(f"hidden{a}_{h}", gated[h], wu_mx[a], v_mx[h]))
+
+        grouped1, dst1 = grouped_tile("wu_grouped1", PACK)
+        round_on_gpsimd(dst1[:, :, :, 3], src1[:, :, :, 3])
+        reorder_plane(1)
+        gated = gates(0)
+        nc.scalar.copy(out=dst1[:, :, :, :3], in_=src1[:, :, :, :3])
+        products(0, 0)
+        back2, dst3 = grouped_tile("wu_grouped3", 1)
+        round_on_gpsimd(dst3[:, :, :, 0], src2[:, :, :, 3])
+        wu_mx.append(quantize_up_weight(1, [grouped1[:]]))
+        products(0, 1)
+        front2, dst2 = grouped_tile("wu_grouped2", 3)
+        round_on_gpsimd(dst2[:, :, :, 2], src2[:, :, :, 2])
+        reorder_plane(2)
+        gated = gates(1)
+        nc.scalar.copy(out=dst2[:, :, :, :2], in_=src2[:, :, :, :2])
+        products(1, 0)
+        wu_mx.append(quantize_up_weight(2, [front2[:, : 2 * PASS], front2[:, 2 * PASS :], back2[:]]))
+        products(1, 1)
+        gated = gates(2)
+        products(2, 0)
+        products(2, 1)
         for h in range(2):
             for n in range(N_TILES):
                 finish(h, n)

@@ -26,15 +26,21 @@ HALF = S // 2
 CHUNK = 128
 RUN = 2
 LAST_PIECE = 128
+SCALAR_ROWS = 64
+GATE_WIDTHS = {(0, 0): (512,), (1, 0): (512,), (2, 1): (128, 128, 256)}
 PLACE = {
-    "wg_raw": 0,
+    "wg_later_raw": 0,
     "wg_plane1": 0,
-    "wu_grouped1": 512,
-    "hidden0_0": 4608,
-    "wu_grouped3": 4608,
-    "hidden0_1": 8704,
-    "wu_grouped2": 8704,
-    "wg_plane2": 11776,
+    "wu_slots1": 1024,
+    "hidden0_0": 5120,
+    "wu_slot2_3": 5120,
+    "hidden0_1": 9216,
+    "wu_slot2_2": 9216,
+    "wg_plane2": 10240,
+    "hidden1_0": 13312,
+    "wu_slots2": 13312,
+    "hidden1_1": 17408,
+    "hidden_lead": 17408,
 }
 
 
@@ -58,14 +64,15 @@ def tile_list_paged_swiglu_residual_kernel(
                 return shared.tile(shape, dtype, name=name, align_bytes=64, offset=PLACE[name])
             return keep.tile(shape, dtype, name=name, tag=name, align_bytes=64)
 
-        wg_raw = placed([P, H // 2], I32, "wg_raw")
+        wg_raw = placed([P, H // 2], I32, "wg_later_raw")
         nc.sync.dma_start(out=wg_raw[:], in_=wg_words[0].bitcast(I32))
+        first_words, later_words = wg_raw[:].bitcast(U16)[:, :PASS], wg_raw[:].bitcast(U16)[:, PASS:]
         offsets = keep.tile([P, S // 16], U16, name="offsets")
         nc.sync.dma_start(offsets[:], offs)
 
         tab_plane = keep.tile([P, T // 4], I32, name="tab_plane", align_bytes=64)
         nc.vector.memset(tab_plane[:], 0)
-        wg_plane_first = keep.tile([P, PASS // 4], I32, name="wg_plane_first", tag="wg_plane_first", align_bytes=64)
+        wg_plane_first = placed([P, PASS // 4], I32, "wg_plane_first")
         nc.vector.memset(wg_plane_first[:], 0)
         wg_plane_rest = keep.tile([P, (H - PASS) // 4], I32, name="wg_plane_rest", align_bytes=64)
         nc.vector.memset(wg_plane_rest[:], 0)
@@ -83,45 +90,34 @@ def tile_list_paged_swiglu_residual_kernel(
         nc.sync.dma_start(out=bias[:], in_=bg.rearrange("(a p t) -> p a t", p=P, t=PACK))
 
         def load_up_weight(first, width):
-            raw = keep.tile([P, PACK * width], F32, name=f"wu_raw{first}", tag=f"wu_raw{first}", align_bytes=64)
+            raw = placed([P, PACK * width], F32, f"wu_raw{first}")
             nc.sync.dma_start(
                 out=raw[:].rearrange("p (j c) -> p j c", j=PACK),
                 in_=wu[:, first : first + width].rearrange("(p j) c -> p j c", j=PACK),
             )
-            return raw
+            return raw[:].rearrange("p (j m t) -> p m j t", j=PACK, t=PACK)
 
         def load_residual_rows(n):
             g_rows = keep.tile([P, T], F32, name=f"g_rows{n}")
             nc.sync.dma_start(out=g_rows[:], in_=gT[n * P : (n + 1) * P, :])
             return g_rows
 
-        wu_raw = [[load_up_weight(0, PASS // 2), load_up_weight(PASS // 2, PASS // 2)]]
-        wu_raw.append([load_up_weight(PASS, PASS)])
+        wu_halves = [load_up_weight(0, PASS // 2), load_up_weight(PASS // 2, PASS // 2)]
+        wu_raw1 = load_up_weight(PASS, PASS)
         load_scale_rows(nc.sync, wg_plane_rest, wg_scales[0].bitcast(I32)[:, PASS // 4 :])
-        wu_raw.append([load_up_weight(2 * PASS, PASS)])
+        wu_raw2 = load_up_weight(2 * PASS, PASS)
         load_scale_rows(nc.sync, wd_plane, wd_scales.bitcast(I32).rearrange("a q c -> q a c"))
         wd_codes = keep.tile([P, R_BLOCKS, N], I32, name="wd_codes", align_bytes=64)
         nc.sync.dma_start(out=wd_codes[:], in_=wd_words.rearrange("a p c i -> p a (c i)").bitcast(I32))
         residual_rows = [load_residual_rows(n) for n in range(N_TILES)]
 
-        def half_list(h):
-            cols = HALF // 16
-            return offsets[:, h * cols : (h + 1) * cols]
+        def listed(first, end):
+            return offsets[:, first // 16 : end // 16]
 
-        v_plane = keep.tile([P, S], U8, name="v_plane", align_bytes=64)
-        nc.vector.tensor_copy(v_plane[:], tab_plane[:].bitcast(U8).indirect(offsets[:]))
-
-        def gather_states(h):
-            plane = v_plane[:, h * HALF : (h + 1) * HALF]
-            codes = keep.tile([P, HALF], U32, name=f"v_codes{h}", tag=("v_codes0", "wg_plane_first")[h], align_bytes=64)
-            pieces = 1
-            width = HALF // pieces
-            for e in range(pieces):
-                cols = slice(e * width // 16, (e + 1) * width // 16)
-                nc.vector.tensor_copy(
-                    codes[:, e * width : (e + 1) * width], tab_codes[:].bitcast(U32).indirect(half_list(h)[:, cols])
-                )
-            return codes, plane
+        def gather_words(h, tag):
+            codes = keep.tile([P, HALF], U32, name=f"v_codes{h}", tag=tag, align_bytes=64)
+            nc.vector.tensor_copy(codes[:], tab_codes[:].bitcast(U32).indirect(listed(h * HALF, (h + 1) * HALF)))
+            return codes
 
         def reorder(engine, ordered, raw):
             engine.tensor_copy(
@@ -129,82 +125,89 @@ def tile_list_paged_swiglu_residual_kernel(
                 in_=raw.rearrange("p (a m t) -> p a t m", t=PACK, m=P),
             )
 
-        def grouped_tile(name, slots):
+        def slots_tile(name, slots):
             tile = placed([P, slots * P * PACK], BF16, name)
             return tile, tile[:].rearrange("p (t m j) -> p m j t", t=slots, j=PACK)
+
+        def round_on_gpsimd(dst, src):
+            walk = "p m j t -> p t m j"
+            nc.gpsimd.tensor_scalar(dst.rearrange(walk), src.rearrange(walk), 1.0, 0.0, MULT, ADD)
 
         def reorder_plane(a):
             plane = placed([P, PASS], U8, f"wg_plane{a}")
             reorder(nc.gpsimd, plane[:], wg_plane_rest[:].bitcast(U8)[:, (a - 1) * PASS : a * PASS])
-            planes.append(plane[:])
+            wg_planes.append(plane[:])
 
-        def raw_view(raw):
-            return raw[:].rearrange("p (j m t) -> p m j t", j=PACK, t=PACK)
-
-        def round_on_gpsimd(dst, src):
-            nc.gpsimd.tensor_scalar(dst, src, 1.0, 0.0, MULT, ADD)
-
-        def quantize_up_weight(a, parts):
-            codes = keep.tile([P, PASS], U32, name=f"wu_codes{a}", align_bytes=64)
-            plane = keep.tile([P, PASS], U8, name=f"wu_plane{a}", align_bytes=64)
-            first = 0
-            for part in parts:
-                end = first + part.shape[1] // PACK
-                nc.vector.quantize_mx(out=codes[:, first:end].bitcast(FP8X4), scales=plane[:, first:end], in_=part)
-                first = end
+        def quantize(name, tag, parts, order):
+            codes = keep.tile([P, PASS], U32, name=f"{name}_codes", tag=tag, align_bytes=64)
+            plane = keep.tile([P, PASS], U8, name=f"{name}_plane", align_bytes=64)
+            firsts = [sum(part.shape[1] for part in parts[:k]) // PACK for k in range(len(parts) + 1)]
+            for k in order:
+                cols = slice(firsts[k], firsts[k + 1])
+                nc.vector.quantize_mx(out=codes[:, cols].bitcast(FP8X4), scales=plane[:, cols], in_=parts[k])
             return codes, plane
 
-        def gate(a, h, wg_mx, v_mx, pieces):
-            if a + h == 0:
-                gated = keep.tile([P, PACK, HALF], F32, name=f"gated{a}", tag=f"wu_raw{a * PASS}", align_bytes=64)
+        def gate(a, h, first, width):
+            if a + h + first == 0:
+                gated = keep.tile([P, PACK, width], F32, name="first_gated", tag="wu_raw0", align_bytes=64)
             else:
-                gated = work.tile([P, PACK, HALF], F32, name="gated", bufs=3)
-            width = HALF // pieces
-            for e in range(pieces):
-                tokens = slice(e * width, (e + 1) * width)
-                for t in range(PACK):
-                    bank = psum.tile([P, HALF], F32, name="wide_bank", bufs=4)
-                    nc.tensor.matmul_mx(
-                        out=bank[:, :width],
-                        lhsT=wg_mx[0].bitcast(U8)[:, 2 * P * t : 2 * P * (t + 1)].bitcast(FP4X4),
-                        lhsT_scale=wg_mx[1][:, P * t : P * (t + 1)],
-                        rhs=v_mx[0][:, tokens].bitcast(FP8X4),
-                        rhs_scale=v_mx[1][:, tokens],
-                        start=True,
-                        stop=True,
-                    )
-                    nc.scalar.activation(
-                        out=gated[:, t, tokens], in_=bank[:, :width], func=SILU, bias=bias[:, a, t : t + 1]
-                    )
-            return gated
+                gated = work.tile([P, PACK, width], F32, name="gated", bufs=4)
+            tokens = slice(first, first + width)
+            for t in range(PACK):
+                bank = psum.tile([P, HALF], F32, name="wide_bank", bufs=4)
+                nc.tensor.matmul_mx(
+                    out=bank[:, :width],
+                    lhsT=wg_codes[a].bitcast(U8)[:, 2 * P * t : 2 * P * (t + 1)].bitcast(FP4X4),
+                    lhsT_scale=wg_planes[a][:, P * t : P * (t + 1)],
+                    rhs=v_codes[h][:, tokens].bitcast(FP8X4),
+                    rhs_scale=v_plane[:, h * HALF + first : h * HALF + first + width],
+                    start=True,
+                    stop=True,
+                )
+                nc.scalar.activation(out=gated[:, t, :], in_=bank[:, :width], func=SILU, bias=bias[:, a, t : t + 1])
+            return [gated[:, :, c : c + CHUNK] for c in range(0, width, CHUNK)]
 
-        def up_and_product(name, gated, wu_mx, v_mx):
-            hidden = placed([P, HALF * PACK], BF16, name)
-            for c in range(HALF // CHUNK):
-                tokens = slice(c * CHUNK, (c + 1) * CHUNK)
-                bank = psum.tile([P, PACK, CHUNK], F32, name="up_bank", bufs=4)
-                for t in range(PACK):
-                    nc.tensor.matmul_mx(
-                        out=bank[:, t, :],
-                        lhsT=wu_mx[0][:, P * t : P * (t + 1)].bitcast(FP8X4),
-                        lhsT_scale=wu_mx[1][:, P * t : P * (t + 1)],
-                        rhs=v_mx[0][:, tokens].bitcast(FP8X4),
-                        rhs_scale=v_mx[1][:, tokens],
-                        start=True,
-                        stop=True,
-                    )
+        def gates(a, h, pieces=slice(None)):
+            widths = GATE_WIDTHS.get((a, h), (HALF,))
+            starts = [(sum(widths[:k]), width) for k, width in enumerate(widths)]
+            return [chunk for first, width in starts[pieces] for chunk in gate(a, h, first, width)]
+
+        def up(a, h, c):
+            bank = psum.tile([P, PACK, CHUNK], F32, name="up_bank", bufs=4)
+            for t in range(PACK):
+                nc.tensor.matmul_mx(
+                    out=bank[:, t, :],
+                    lhsT=wu_mx[a][0][:, P * t : P * (t + 1)].bitcast(FP8X4),
+                    lhsT_scale=wu_mx[a][1][:, P * t : P * (t + 1)],
+                    rhs=v_codes[h][:, c * CHUNK : (c + 1) * CHUNK].bitcast(FP8X4),
+                    rhs_scale=v_plane[:, h * HALF + c * CHUNK : h * HALF + (c + 1) * CHUNK],
+                    start=True,
+                    stop=True,
+                )
+            return bank
+
+        def products(a, h, gated, first_chunk=0):
+            hidden = placed([P, HALF * PACK], BF16, f"hidden{a}_{h}")
+            for c in range(first_chunk, HALF // CHUNK):
                 nc.vector.tensor_tensor(
-                    out=hidden[:, c * CHUNK * PACK : (c + 1) * CHUNK * PACK].rearrange(
-                        "p (g i t) -> p g t i", i=RUN, t=PACK
-                    ),
-                    in0=bank[:].rearrange("p t (g i) -> p g t i", i=RUN),
-                    in1=gated[:, :, tokens].rearrange("p t (g i) -> p g t i", i=RUN),
+                    out=hidden[:, c * PASS : (c + 1) * PASS].rearrange("p (g i t) -> p g t i", i=RUN, t=PACK),
+                    in0=up(a, h, c)[:].rearrange("p t (g i) -> p g t i", i=RUN),
+                    in1=gated[c].rearrange("p t (g i) -> p g t i", i=RUN),
                     op=MULT,
                 )
-            codes = work.tile([P, HALF], U32, name="h_codes", bufs=2 * R_BLOCKS, align_bytes=64)
-            plane = work.tile([P, HALF], U8, name="h_plane", bufs=2 * R_BLOCKS, align_bytes=64)
-            nc.vector.quantize_mx(out=codes[:].bitcast(FP8X4), scales=plane[:], in_=hidden[:])
-            return codes, plane
+            return hidden
+
+        def product_on_gpsimd(a, h, gated):
+            copied = keep.tile([P, CHUNK, PACK], F32, name="up_copied")
+            nc.scalar.copy(out=copied[:], in_=up(a, h, 0)[:].rearrange("p t c -> p c t"))
+            lead = placed([P, PASS], BF16, "hidden_lead")
+            nc.gpsimd.tensor_tensor(
+                out=lead[:].rearrange("p (c t) -> p c t", t=PACK),
+                in0=copied[:],
+                in1=gated[0].rearrange("p t c -> p c t"),
+                op=MULT,
+            )
+            return lead
 
         def down(n, h_mx):
             bank = psum.tile([P, HALF], F32, name="wide_bank", bufs=4)
@@ -226,57 +229,65 @@ def tile_list_paged_swiglu_residual_kernel(
             result = keep.tile([P, HALF], F32, name=f"result{h}_{n}")
             cuts = (0, HALF - LAST_PIECE, HALF) if (h, n) == (1, N_TILES - 1) else (0, HALF)
             for first, end in zip(cuts, cuts[1:]):
-                picked = residual_rows[n][:].indirect(half_list(h)[:, first // 16 : end // 16])
+                picked = residual_rows[n][:].indirect(listed(h * HALF + first, h * HALF + end))
                 nc.vector.tensor_tensor(result[:, first:end], picked, product[:, first:end], ADD)
                 nc.sync.dma_start(
                     out=out[n * P : (n + 1) * P, h * HALF + first : h * HALF + end], in_=result[:, first:end]
                 )
 
-        v_mx = [gather_states(0)]
+        v_plane = keep.tile([P, S], U8, name="v_plane", align_bytes=64)
+        nc.vector.tensor_copy(v_plane[:], tab_plane[:].bitcast(U8).indirect(offsets[:]))
+        v_codes = [gather_words(0, "v_codes0")]
         first_codes = keep.tile([P, PASS], U16, name="first_codes", align_bytes=64)
-        reorder(nc.vector, first_codes[:], wg_raw[:].bitcast(U16)[:, :PASS])
+        reorder(nc.vector, first_codes[:], first_words)
         first_plane = keep.tile([P, PASS], U8, name="first_plane", align_bytes=64)
         reorder(nc.vector, first_plane[:], wg_plane_first[:].bitcast(U8))
-        grouped, dst = grouped_tile("wu_grouped0", PACK)
-        nc.scalar.copy(out=dst[:, : P // 2], in_=raw_view(wu_raw[0][0]))
-        nc.vector.tensor_copy(out=dst[:, P // 2 :], in_=raw_view(wu_raw[0][1]))
-        wu_mx = [quantize_up_weight(0, [grouped[:, t * PASS : (t + 1) * PASS] for t in range(PACK)])]
-        v_mx.append(gather_states(1))
-
+        slots0, dst = slots_tile("wu_slots0", PACK)
+        nc.scalar.copy(out=dst[:, : P // 2], in_=wu_halves[0])
+        nc.vector.tensor_copy(out=dst[:, SCALAR_ROWS:], in_=wu_halves[1][:, SCALAR_ROWS - P // 2 :])
+        wu_mx = [quantize("wu0", "wu0", [slots0[:, t * PASS : (t + 1) * PASS] for t in range(PACK)], range(PACK))]
+        v_codes.append(gather_words(1, "wg_plane_first"))
+        later_codes = keep.tile([P, H - PASS], U16, name="later_codes", tag="wu_slots0", align_bytes=64)
+        reorder(nc.vector, later_codes[:], later_words)
+        wg_codes = [first_codes[:], later_codes[:, :PASS], later_codes[:, PASS:]]
+        wg_planes = [first_plane[:]]
         h_mx = ([], [])
-        later = keep.tile([P, H - PASS], U16, name="later_codes", tag="wu_grouped0", align_bytes=64)
-        reorder(nc.vector, later[:], wg_raw[:].bitcast(U16)[:, PASS:])
-        codes = [first_codes[:], later[:, :PASS], later[:, PASS:]]
-        planes = [first_plane[:]]
-        src1, src2 = raw_view(wu_raw[1][0]), raw_view(wu_raw[2][0])
 
-        def gates(a):
-            return [gate(a, h, (codes[a], planes[a]), v_mx[h], 1) for h in range(2)]
+        def whole(a, h, hidden, tag=None):
+            h_mx[h].append(quantize(f"h{a}_{h}", tag or f"h{a}_{h}", [hidden[:]], (0,)))
 
-        def products(a, h):
-            h_mx[h].append(up_and_product(f"hidden{a}_{h}", gated[h], wu_mx[a], v_mx[h]))
-
-        grouped1, dst1 = grouped_tile("wu_grouped1", PACK)
-        round_on_gpsimd(dst1[:, :, :, 3], src1[:, :, :, 3])
+        slots1, dst1 = slots_tile("wu_slots1", PACK)
+        round_on_gpsimd(dst1[:, :, :, 3:], wu_raw1[:, :, :, 3:])
         reorder_plane(1)
-        gated = gates(0)
-        nc.scalar.copy(out=dst1[:, :, :, :3], in_=src1[:, :, :, :3])
-        products(0, 0)
-        back2, dst3 = grouped_tile("wu_grouped3", 1)
-        round_on_gpsimd(dst3[:, :, :, 0], src2[:, :, :, 3])
-        wu_mx.append(quantize_up_weight(1, [grouped1[:]]))
-        products(0, 1)
-        front2, dst2 = grouped_tile("wu_grouped2", 3)
-        round_on_gpsimd(dst2[:, :, :, 2], src2[:, :, :, 2])
+        gated = [gates(0, 0), gates(0, 1)]
+        nc.scalar.copy(out=dst1[:, :, :, :3], in_=wu_raw1[:, :, :, :3])
+        whole(0, 0, products(0, 0, gated[0]))
+
+        slot3, dst = slots_tile("wu_slot2_3", 1)
+        round_on_gpsimd(dst, wu_raw2[:, :, :, 3:])
+        hidden = products(0, 1, gated[1])
+        wu_mx.append(quantize("wu1", "wu1", [slots1[:]], (0,)))
+        whole(0, 1, hidden, f"wu_raw{PASS}")
+
+        slot2, dst = slots_tile("wu_slot2_2", 1)
+        round_on_gpsimd(dst, wu_raw2[:, :, :, 2:3])
         reorder_plane(2)
-        gated = gates(1)
-        nc.scalar.copy(out=dst2[:, :, :, :2], in_=src2[:, :, :, :2])
-        products(1, 0)
-        wu_mx.append(quantize_up_weight(2, [front2[:, : 2 * PASS], front2[:, 2 * PASS :], back2[:]]))
-        products(1, 1)
-        gated = gates(2)
-        products(2, 0)
-        products(2, 1)
+        gated = [gates(1, 0), gates(1, 1)]
+        slots2, dst = slots_tile("wu_front2", 2)
+        nc.scalar.copy(out=dst, in_=wu_raw2[:, :, :, :2])
+        whole(1, 0, products(1, 0, gated[0]))
+
+        wu_mx.append(quantize("wu2", f"wu_raw{2 * PASS}", [slots2[:], slot2[:], slot3[:]], range(3)))
+        whole(1, 1, products(1, 1, gated[1]))
+
+        gated = [gates(2, 0), gates(2, 1, slice(0, 1))]
+        lead = product_on_gpsimd(2, 1, gated[1])
+        gated[1].extend(gates(2, 1, slice(1, None)))
+        whole(2, 0, products(2, 0, gated[0]))
+        hidden = products(2, 1, gated[1], first_chunk=1)
+        parts = [lead[:], hidden[:, PASS : 2 * PASS], hidden[:, 2 * PASS :]]
+        h_mx[1].append(quantize("h2_1", "h2_1", parts, range(3)))
+
         for h in range(2):
             for n in range(N_TILES):
                 finish(h, n)

@@ -29,18 +29,15 @@ LAST_PIECE = 128
 SCALAR_ROWS = 64
 GATE_WIDTHS = {(0, 0): (512,), (1, 0): (512,), (2, 1): (128, 128, 256)}
 PLACE = {
-    "wg_later_raw": 0,
+    "wu_slots0": 0,
     "wg_plane1": 0,
     "wu_slots1": 1024,
+    "wu_slot2_2": 1024,
+    "wg_plane2": 2048,
     "hidden0_0": 5120,
     "wu_slot2_3": 5120,
-    "hidden0_1": 9216,
-    "wu_slot2_2": 9216,
-    "wg_plane2": 10240,
-    "hidden1_0": 13312,
-    "wu_slots2": 13312,
-    "hidden1_1": 17408,
-    "hidden_lead": 17408,
+    "hidden1_1": 9216,
+    "hidden_lead": 9216,
 }
 
 
@@ -186,7 +183,7 @@ def tile_list_paged_swiglu_residual_kernel(
                 )
             return bank
 
-        def products(a, h, gated, first_chunk=0):
+        def products(a, h, gated, first_chunk=0, between=None):
             hidden = placed([P, HALF * PACK], BF16, f"hidden{a}_{h}")
             for c in range(first_chunk, HALF // CHUNK):
                 nc.vector.tensor_tensor(
@@ -195,6 +192,8 @@ def tile_list_paged_swiglu_residual_kernel(
                     in1=gated[c].rearrange("p t (g i) -> p g t i", i=RUN),
                     op=MULT,
                 )
+                if c == 1 and between is not None:
+                    between()
             return hidden
 
         def product_on_gpsimd(a, h, gated):
@@ -247,7 +246,7 @@ def tile_list_paged_swiglu_residual_kernel(
         nc.vector.tensor_copy(out=dst[:, SCALAR_ROWS:], in_=wu_halves[1][:, SCALAR_ROWS - P // 2 :])
         wu_mx = [quantize("wu0", "wu0", [slots0[:, t * PASS : (t + 1) * PASS] for t in range(PACK)], range(PACK))]
         v_codes.append(gather_words(1, "wg_plane_first"))
-        later_codes = keep.tile([P, H - PASS], U16, name="later_codes", tag="wu_slots0", align_bytes=64)
+        later_codes = keep.tile([P, H - PASS], U16, name="later_codes", tag="wu_raw256", align_bytes=64)
         reorder(nc.vector, later_codes[:], later_words)
         wg_codes = [first_codes[:], later_codes[:, :PASS], later_codes[:, PASS:]]
         wg_planes = [first_plane[:]]
@@ -277,8 +276,11 @@ def tile_list_paged_swiglu_residual_kernel(
         nc.scalar.copy(out=dst, in_=wu_raw2[:, :, :, :2])
         whole(1, 0, products(1, 0, gated[0]))
 
-        wu_mx.append(quantize("wu2", f"wu_raw{2 * PASS}", [slots2[:], slot2[:], slot3[:]], range(3)))
-        whole(1, 1, products(1, 1, gated[1]))
+
+        def last_up_weight():
+            wu_mx.append(quantize("wu2", f"wu_raw{2 * PASS}", [slots2[:], slot2[:], slot3[:]], range(3)))
+
+        whole(1, 1, products(1, 1, gated[1], between=last_up_weight))
 
         gated = [gates(2, 0), gates(2, 1, slice(0, 1))]
         lead = product_on_gpsimd(2, 1, gated[1])

@@ -26,6 +26,7 @@ HALF = S // 2
 CHUNK = 128
 RUN = 2
 LAST_PIECE = 128
+SECOND_SCALAR_ROWS = 40
 SCALAR_ROWS = 64
 GATE_WIDTHS = {(0, 0): (512,), (1, 0): (512,), (2, 1): (128, 128, 256)}
 PLACE = {
@@ -127,7 +128,7 @@ def tile_list_paged_swiglu_residual_kernel(
             return tile, tile[:].rearrange("p (t m j) -> p m j t", t=slots, j=PACK)
 
         def round_on_gpsimd(dst, src):
-            walk = "p m j t -> p t m j"
+            walk = "p m j t -> p m t j"
             nc.gpsimd.tensor_scalar(dst.rearrange(walk), src.rearrange(walk), 1.0, 0.0, MULT, ADD)
 
         def reorder_plane(a):
@@ -256,10 +257,10 @@ def tile_list_paged_swiglu_residual_kernel(
             h_mx[h].append(quantize(f"h{a}_{h}", tag or f"h{a}_{h}", [hidden[:]], (0,)))
 
         slots1, dst1 = slots_tile("wu_slots1", PACK)
-        round_on_gpsimd(dst1[:, :, :, 3:], wu_raw1[:, :, :, 3:])
+        round_on_gpsimd(dst1[:, SECOND_SCALAR_ROWS:], wu_raw1[:, SECOND_SCALAR_ROWS:])
         reorder_plane(1)
         gated = [gates(0, 0), gates(0, 1)]
-        nc.scalar.copy(out=dst1[:, :, :, :3], in_=wu_raw1[:, :, :, :3])
+        nc.scalar.copy(out=dst1[:, :SECOND_SCALAR_ROWS], in_=wu_raw1[:, :SECOND_SCALAR_ROWS])
         whole(0, 0, products(0, 0, gated[0]))
 
         slot3, dst = slots_tile("wu_slot2_3", 1)

@@ -33,12 +33,17 @@ PLACE = {
     "wu_slots0": 0,
     "wg_plane1": 0,
     "wu_slots1": 1024,
-    "wu_slot2_2": 1024,
+    "wu_upper2": 2560,
     "wg_plane2": 2048,
     "hidden0_0": 5120,
-    "wu_slot2_3": 5120,
+    "wu_early2": 5120,
     "hidden1_1": 9216,
-    "hidden_lead": 9216,
+    "lead2": 9216,
+    "lead1": 2560,
+    "gated1_1": 14336,
+    "wu_raw1024": 20480,
+    "up_copied1": 24576,
+    "h1_1_codes": 24576,
 }
 
 
@@ -103,7 +108,7 @@ def tile_list_paged_swiglu_residual_kernel(
         wu_halves = [load_up_weight(0, PASS // 2), load_up_weight(PASS // 2, PASS // 2)]
         wu_raw1 = load_up_weight(PASS, PASS)
         load_scale_rows(nc.sync, wg_plane_rest, wg_scales[0].bitcast(I32)[:, PASS // 4 :])
-        wu_raw2 = load_up_weight(2 * PASS, PASS)
+        last_halves = [load_up_weight(2 * PASS + first, PASS // 2) for first in (0, PASS // 2)]
         load_scale_rows(nc.sync, wd_plane, wd_scales.bitcast(I32).rearrange("a q c -> q a c"))
         wd_codes = keep.tile([P, R_BLOCKS, N], I32, name="wd_codes", align_bytes=64)
         nc.sync.dma_start(out=wd_codes[:], in_=wd_words.rearrange("a p c i -> p a (c i)").bitcast(I32))
@@ -123,8 +128,8 @@ def tile_list_paged_swiglu_residual_kernel(
                 in_=raw.rearrange("p (a m t) -> p a t m", t=PACK, m=P),
             )
 
-        def slots_tile(name, slots):
-            tile = placed([P, slots * P * PACK], BF16, name)
+        def slots_tile(name, slots, groups=P):
+            tile = placed([P, slots * groups * PACK], BF16, name)
             return tile, tile[:].rearrange("p (t m j) -> p m j t", t=slots, j=PACK)
 
         def round_on_gpsimd(dst, src):
@@ -137,7 +142,10 @@ def tile_list_paged_swiglu_residual_kernel(
             wg_planes.append(plane[:])
 
         def quantize(name, tag, parts, order):
-            codes = keep.tile([P, PASS], U32, name=f"{name}_codes", tag=tag, align_bytes=64)
+            if f"{name}_codes" in PLACE:
+                codes = placed([P, PASS], U32, f"{name}_codes")
+            else:
+                codes = keep.tile([P, PASS], U32, name=f"{name}_codes", tag=tag, align_bytes=64)
             plane = keep.tile([P, PASS], U8, name=f"{name}_plane", align_bytes=64)
             firsts = [sum(part.shape[1] for part in parts[:k]) // PACK for k in range(len(parts) + 1)]
             for k in order:
@@ -148,13 +156,20 @@ def tile_list_paged_swiglu_residual_kernel(
         def gate(a, h, first, width):
             if a + h + first == 0:
                 gated = keep.tile([P, PACK, width], F32, name="first_gated", tag="wu_raw0", align_bytes=64)
+            elif f"gated{a}_{h}" in PLACE:
+                gated = placed([P, PACK, width], F32, f"gated{a}_{h}")
             else:
                 gated = work.tile([P, PACK, width], F32, name="gated", bufs=4)
             tokens = slice(first, first + width)
+            if width == CHUNK:
+                one_bank = psum.tile([P, PACK, CHUNK], F32, name="wide_bank", bufs=4)
             for t in range(PACK):
-                bank = psum.tile([P, HALF], F32, name="wide_bank", bufs=4)
+                if width == CHUNK:
+                    bank = one_bank[:, t, :]
+                else:
+                    bank = psum.tile([P, HALF], F32, name="wide_bank", bufs=4)[:, :width]
                 nc.tensor.matmul_mx(
-                    out=bank[:, :width],
+                    out=bank,
                     lhsT=wg_codes[a].bitcast(U8)[:, 2 * P * t : 2 * P * (t + 1)].bitcast(FP4X4),
                     lhsT_scale=wg_planes[a][:, P * t : P * (t + 1)],
                     rhs=v_codes[h][:, tokens].bitcast(FP8X4),
@@ -162,7 +177,13 @@ def tile_list_paged_swiglu_residual_kernel(
                     start=True,
                     stop=True,
                 )
-                nc.scalar.activation(out=gated[:, t, :], in_=bank[:, :width], func=SILU, bias=bias[:, a, t : t + 1])
+                if width > CHUNK:
+                    nc.scalar.activation(out=gated[:, t, :], in_=bank, func=SILU, bias=bias[:, a, t : t + 1])
+            if width == CHUNK:
+                for t in range(PACK):
+                    nc.scalar.activation(
+                        out=gated[:, t, :], in_=one_bank[:, t, :], func=SILU, bias=bias[:, a, t : t + 1]
+                    )
             return [gated[:, :, c : c + CHUNK] for c in range(0, width, CHUNK)]
 
         def gates(a, h, pieces=slice(None)):
@@ -184,7 +205,7 @@ def tile_list_paged_swiglu_residual_kernel(
                 )
             return bank
 
-        def products(a, h, gated, first_chunk=0, between=None):
+        def products(a, h, gated, first_chunk=0):
             hidden = placed([P, HALF * PACK], BF16, f"hidden{a}_{h}")
             for c in range(first_chunk, HALF // CHUNK):
                 nc.vector.tensor_tensor(
@@ -193,14 +214,15 @@ def tile_list_paged_swiglu_residual_kernel(
                     in1=gated[c].rearrange("p t (g i) -> p g t i", i=RUN),
                     op=MULT,
                 )
-                if c == 1 and between is not None:
-                    between()
             return hidden
 
-        def product_on_gpsimd(a, h, gated):
-            copied = keep.tile([P, CHUNK, PACK], F32, name="up_copied")
+        def copy_first_up(a, h):
+            copied = placed([P, CHUNK, PACK], F32, f"up_copied{a}")
             nc.scalar.copy(out=copied[:], in_=up(a, h, 0)[:].rearrange("p t c -> p c t"))
-            lead = placed([P, PASS], BF16, "hidden_lead")
+            return copied
+
+        def product_on_gpsimd(a, copied, gated):
+            lead = placed([P, PASS], BF16, f"lead{a}")
             nc.gpsimd.tensor_tensor(
                 out=lead[:].rearrange("p (c t) -> p c t", t=PACK),
                 in0=copied[:],
@@ -263,33 +285,39 @@ def tile_list_paged_swiglu_residual_kernel(
         nc.scalar.copy(out=dst1[:, :SECOND_SCALAR_ROWS], in_=wu_raw1[:, :SECOND_SCALAR_ROWS])
         whole(0, 0, products(0, 0, gated[0]))
 
-        slot3, dst = slots_tile("wu_slot2_3", 1)
-        round_on_gpsimd(dst, wu_raw2[:, :, :, 3:])
+        early2, dst = slots_tile("wu_early2", 2, P // 2)
+        round_on_gpsimd(dst, last_halves[0][:, :, :, 2:])
         hidden = products(0, 1, gated[1])
         wu_mx.append(quantize("wu1", "wu1", [slots1[:]], (0,)))
         whole(0, 1, hidden, f"wu_raw{PASS}")
 
-        slot2, dst = slots_tile("wu_slot2_2", 1)
-        round_on_gpsimd(dst, wu_raw2[:, :, :, 2:3])
         reorder_plane(2)
-        gated = [gates(1, 0), gates(1, 1)]
-        slots2, dst = slots_tile("wu_front2", 2)
-        nc.scalar.copy(out=dst, in_=wu_raw2[:, :, :, :2])
-        whole(1, 0, products(1, 0, gated[0]))
+        upper2, dst = slots_tile("wu_upper2", PACK, P // 2)
+        round_on_gpsimd(dst, last_halves[1])
+        gated = [gates(1, 0)]
+        front2, dst = slots_tile("wu_front2", 2, P // 2)
+        nc.scalar.copy(out=dst, in_=last_halves[0][:, :, :, :2])
+        hidden = products(1, 0, gated[0])
+        copied = copy_first_up(1, 1)
+        gated.append(gates(1, 1))
+        lower = [tile[:, t * 256 : (t + 1) * 256] for tile in (front2, early2) for t in range(2)]
+        parts = [part for t in range(PACK) for part in (lower[t], upper2[:, t * 256 : (t + 1) * 256])]
+        wu_mx.append(quantize("wu2", f"wu_raw{2 * PASS + PASS // 2}", parts, range(2 * PACK)))
+        whole(1, 0, hidden)
 
+        def shared_unit(a, lead, hidden):
+            parts = [lead[:], hidden[:, PASS : 2 * PASS], hidden[:, 2 * PASS :]]
+            h_mx[1].append(quantize(f"h{a}_1", f"h{a}_1", parts, range(3)))
 
-        def last_up_weight():
-            wu_mx.append(quantize("wu2", f"wu_raw{2 * PASS}", [slots2[:], slot2[:], slot3[:]], range(3)))
-
-        whole(1, 1, products(1, 1, gated[1], between=last_up_weight))
-
+        lead = product_on_gpsimd(1, copied, gated[1])
+        hidden = products(1, 1, gated[1], first_chunk=1)
         gated = [gates(2, 0), gates(2, 1, slice(0, 1))]
-        lead = product_on_gpsimd(2, 1, gated[1])
+        shared_unit(1, lead, hidden)
+
+        lead = product_on_gpsimd(2, copy_first_up(2, 1), gated[1])
         gated[1].extend(gates(2, 1, slice(1, None)))
         whole(2, 0, products(2, 0, gated[0]))
-        hidden = products(2, 1, gated[1], first_chunk=1)
-        parts = [lead[:], hidden[:, PASS : 2 * PASS], hidden[:, 2 * PASS :]]
-        h_mx[1].append(quantize("h2_1", "h2_1", parts, range(3)))
+        shared_unit(2, lead, products(2, 1, gated[1], first_chunk=1))
 
         for h in range(2):
             for n in range(N_TILES):

@@ -24,26 +24,24 @@ R_BLOCKS = H // PASS
 N_TILES = N // P
 HALF = S // 2
 CHUNK = 128
+CHUNKS = HALF // CHUNK
 RUN = 2
 LAST_PIECE = 128
-SECOND_SCALAR_ROWS = 40
-SCALAR_ROWS = 64
-GATE_WIDTHS = {(0, 0): (512,), (1, 0): (512,), (2, 1): (128, 128, 256)}
+SCALAR_GROUPS = (64, 32, 32)
+EARLY_SCALES = HALF
+EARLY_COLUMNS = 640
 PLACE = {
+    "first_raw": 8192,
+    "late_scales": 8192,
+    "wu_back0": 10240,
+    "wg_plane2": 10240,
+    "v_codes1": 10752,
     "wu_slots0": 0,
-    "wg_plane1": 0,
     "wu_slots1": 1024,
-    "wu_upper2": 2560,
-    "wg_plane2": 2048,
-    "hidden0_0": 5120,
-    "wu_early2": 5120,
-    "hidden1_1": 9216,
-    "lead2": 9216,
-    "lead1": 2560,
-    "gated1_1": 14336,
-    "wu_raw1024": 20480,
-    "up_copied1": 24576,
-    "h1_1_codes": 24576,
+    "wu_slots2": 1024,
+    "lead0": 1024,
+    "lead1": 1024,
+    "lead2": 1024,
 }
 
 
@@ -58,138 +56,157 @@ def tile_list_paged_swiglu_residual_kernel(
     nc = tc.nc
     with ExitStack() as ctx:
         keep = ctx.enter_context(tc.tile_pool(name="keep", bufs=1))
-        shared = ctx.enter_context(tc.tile_pool(name="shared", bufs=1))
-        work = ctx.enter_context(tc.tile_pool(name="work", bufs=2))
         psum = ctx.enter_context(tc.psum_pool(name="psum", bufs=1))
 
-        def placed(shape, dtype, name):
+        shared = ctx.enter_context(tc.tile_pool(name="shared", bufs=1))
+
+        def sbuf(shape, dtype, name, tag=None):
             if name in PLACE:
                 return shared.tile(shape, dtype, name=name, align_bytes=64, offset=PLACE[name])
-            return keep.tile(shape, dtype, name=name, tag=name, align_bytes=64)
+            return keep.tile(shape, dtype, name=name, tag=tag or name, align_bytes=64)
 
-        wg_raw = placed([P, H // 2], I32, "wg_later_raw")
-        nc.sync.dma_start(out=wg_raw[:], in_=wg_words[0].bitcast(I32))
-        first_words, later_words = wg_raw[:].bitcast(U16)[:, :PASS], wg_raw[:].bitcast(U16)[:, PASS:]
+        tab_codes = sbuf([P, T], I32, "tab_codes")
+        tab_rows = tab_words[0].rearrange("p t i -> p (t i)").bitcast(I32)
+        nc.sync.dma_start(out=tab_codes[:, :EARLY_COLUMNS], in_=tab_rows[:, :EARLY_COLUMNS])
+        bias = keep.tile([P, R_BLOCKS, PACK], F32, name="bias")
+        nc.sync.dma_start(out=bias[:], in_=bg.rearrange("(a p t) -> p a t", p=P, t=PACK))
         offsets = keep.tile([P, S // 16], U16, name="offsets")
         nc.sync.dma_start(offsets[:], offs)
 
-        tab_plane = keep.tile([P, T // 4], I32, name="tab_plane", align_bytes=64)
+        tab_plane = sbuf([P, T // 4], I32, "tab_plane")
         nc.vector.memset(tab_plane[:], 0)
-        wg_plane_first = placed([P, PASS // 4], I32, "wg_plane_first")
-        nc.vector.memset(wg_plane_first[:], 0)
-        wg_plane_rest = keep.tile([P, (H - PASS) // 4], I32, name="wg_plane_rest", align_bytes=64)
-        nc.vector.memset(wg_plane_rest[:], 0)
-        wd_plane = keep.tile([P, R_BLOCKS, N // 4], I32, name="wd_plane", align_bytes=64)
+        wg_raw_plane = sbuf([P, H // 4], I32, "wg_raw_plane")
+        nc.vector.memset(wg_raw_plane[:], 0)
+        wd_plane = sbuf([P, R_BLOCKS, N // 4], I32, "wd_plane")
         nc.vector.memset(wd_plane[:], 0)
         warm = keep.tile([P, 2], F32, name="warm")
         nc.vector.memset(warm[:, 0:1], 0.0)
         nc.scalar.activation(out=warm[:, 1:2], in_=warm[:, 0:1], func=SILU)
 
         load_scale_rows(nc.sync, tab_plane, tab_scales[0].bitcast(I32))
-        tab_codes = keep.tile([P, T], I32, name="tab_codes", align_bytes=64)
-        nc.sync.dma_start(out=tab_codes[:], in_=tab_words[0].rearrange("p t i -> p (t i)").bitcast(I32))
-        load_scale_rows(nc.sync, wg_plane_first, wg_scales[0].bitcast(I32)[:, : PASS // 4])
-        bias = keep.tile([P, R_BLOCKS, PACK], F32, name="bias")
-        nc.sync.dma_start(out=bias[:], in_=bg.rearrange("(a p t) -> p a t", p=P, t=PACK))
+        nc.sync.dma_start(out=tab_codes[:, EARLY_COLUMNS:], in_=tab_rows[:, EARLY_COLUMNS:])
+        load_scale_rows(nc.sync, wg_raw_plane, wg_scales[0].bitcast(I32))
+        first_raw = sbuf([P, PASS // 2], I32, "first_raw")
+        nc.sync.dma_start(out=first_raw[:], in_=wg_words[0].bitcast(I32)[:, : PASS // 2])
+        later_raw = sbuf([P, (H - PASS) // 2], I32, "later_raw")
+        nc.sync.dma_start(out=later_raw[:], in_=wg_words[0].bitcast(I32)[:, PASS // 2 :])
 
-        def load_up_weight(first, width):
-            raw = placed([P, PACK * width], F32, f"wu_raw{first}")
+        def load_up_weight(name, first, width):
+            raw = sbuf([P, PACK * width], F32, name)
             nc.sync.dma_start(
                 out=raw[:].rearrange("p (j c) -> p j c", j=PACK),
                 in_=wu[:, first : first + width].rearrange("(p j) c -> p j c", j=PACK),
             )
             return raw[:].rearrange("p (j m t) -> p m j t", j=PACK, t=PACK)
 
-        def load_residual_rows(n):
+        wu_raw = []
+        for a, groups in enumerate(SCALAR_GROUPS):
+            cut = PACK * groups
+            wu_raw.append(
+                (
+                    load_up_weight(f"wu_front{a}", a * PASS, cut),
+                    load_up_weight(f"wu_back{a}", a * PASS + cut, PASS - cut),
+                )
+            )
+        load_scale_rows(nc.sync, wd_plane, wd_scales.bitcast(I32).rearrange("a q c -> q a c"))
+        wd_codes = sbuf([P, R_BLOCKS, N], I32, "wd_codes")
+        nc.sync.dma_start(out=wd_codes[:], in_=wd_words.rearrange("a p c i -> p a (c i)").bitcast(I32))
+        residual_rows = []
+        for n in range(N_TILES):
             g_rows = keep.tile([P, T], F32, name=f"g_rows{n}")
             nc.sync.dma_start(out=g_rows[:], in_=gT[n * P : (n + 1) * P, :])
-            return g_rows
-
-        wu_halves = [load_up_weight(0, PASS // 2), load_up_weight(PASS // 2, PASS // 2)]
-        wu_raw1 = load_up_weight(PASS, PASS)
-        load_scale_rows(nc.sync, wg_plane_rest, wg_scales[0].bitcast(I32)[:, PASS // 4 :])
-        last_halves = [load_up_weight(2 * PASS + first, PASS // 2) for first in (0, PASS // 2)]
-        load_scale_rows(nc.sync, wd_plane, wd_scales.bitcast(I32).rearrange("a q c -> q a c"))
-        wd_codes = keep.tile([P, R_BLOCKS, N], I32, name="wd_codes", align_bytes=64)
-        nc.sync.dma_start(out=wd_codes[:], in_=wd_words.rearrange("a p c i -> p a (c i)").bitcast(I32))
-        residual_rows = [load_residual_rows(n) for n in range(N_TILES)]
+            residual_rows.append(g_rows)
 
         def listed(first, end):
             return offsets[:, first // 16 : end // 16]
 
-        def gather_words(h, tag):
-            codes = keep.tile([P, HALF], U32, name=f"v_codes{h}", tag=tag, align_bytes=64)
-            nc.vector.tensor_copy(codes[:], tab_codes[:].bitcast(U32).indirect(listed(h * HALF, (h + 1) * HALF)))
-            return codes
+        def gather_words(h, first, end):
+            picked = tab_codes[:].bitcast(U32).indirect(listed(h * HALF + first, h * HALF + end))
+            nc.vector.tensor_copy(v_codes[h][:, first:end], picked)
 
-        def reorder(engine, ordered, raw):
-            engine.tensor_copy(
-                out=ordered.rearrange("p (a t m) -> p a t m", t=PACK, m=P),
-                in_=raw.rearrange("p (a m t) -> p a t m", t=PACK, m=P),
-            )
+        def gather_scales(name, first, end):
+            plane = sbuf([P, end - first], U8, name)
+            nc.vector.tensor_copy(plane[:], tab_plane[:].bitcast(U8).indirect(listed(first, end)))
+            return plane
 
-        def slots_tile(name, slots, groups=P):
-            tile = placed([P, slots * groups * PACK], BF16, name)
-            return tile, tile[:].rearrange("p (t m j) -> p m j t", t=slots, j=PACK)
+        def token_scales(first, width):
+            if first < EARLY_SCALES:
+                return early_scales[:, first : first + width]
+            return late_scales[:, first - EARLY_SCALES : first - EARLY_SCALES + width]
 
-        def round_on_gpsimd(dst, src):
-            walk = "p m j t -> p m t j"
-            nc.gpsimd.tensor_scalar(dst.rearrange(walk), src.rearrange(walk), 1.0, 0.0, MULT, ADD)
+        def dealt(ordered, raw):
+            return {
+                "out": ordered.rearrange("p (a t m) -> p a t m", t=PACK, m=P),
+                "in_": raw.rearrange("p (a m t) -> p a t m", t=PACK, m=P),
+            }
 
-        def reorder_plane(a):
-            plane = placed([P, PASS], U8, f"wg_plane{a}")
-            reorder(nc.gpsimd, plane[:], wg_plane_rest[:].bitcast(U8)[:, (a - 1) * PASS : a * PASS])
-            wg_planes.append(plane[:])
+        def deal_plane(a):
+            plane = sbuf([P, PASS], U8, f"wg_plane{a}")
+            nc.vector.tensor_copy(**dealt(plane[:], wg_raw_plane[:].bitcast(U8)[:, a * PASS : (a + 1) * PASS]))
+            return plane[:]
 
-        def quantize(name, tag, parts, order):
-            if f"{name}_codes" in PLACE:
-                codes = placed([P, PASS], U32, f"{name}_codes")
+        def round_up_weight(a):
+            slots = sbuf([P, PASS * PACK], BF16, f"wu_slots{a}", "staged")
+            dst = slots[:].rearrange("p (t m j) -> p m j t", t=PACK, j=PACK)
+            cut = SCALAR_GROUPS[a]
+            front, back = wu_raw[a]
+            nc.scalar.copy(out=dst[:, :cut], in_=front)
+            if a == 0:
+                for pair in (slice(0, 2), slice(2, 4)):
+                    nc.vector.tensor_copy(out=dst[:, cut:, :, pair], in_=back[:, :, :, pair])
             else:
-                codes = keep.tile([P, PASS], U32, name=f"{name}_codes", tag=tag, align_bytes=64)
-            plane = keep.tile([P, PASS], U8, name=f"{name}_plane", align_bytes=64)
-            firsts = [sum(part.shape[1] for part in parts[:k]) // PACK for k in range(len(parts) + 1)]
-            for k in order:
-                cols = slice(firsts[k], firsts[k + 1])
-                nc.vector.quantize_mx(out=codes[:, cols].bitcast(FP8X4), scales=plane[:, cols], in_=parts[k])
+                walk = "p m j t -> p m t j"
+                nc.gpsimd.tensor_scalar(dst[:, cut:].rearrange(walk), back.rearrange(walk), 1.0, 0.0, MULT, ADD)
+            return slots
+
+        def quantize(name, parts, tag=None):
+            codes = sbuf([P, PASS], U32, f"{name}_codes", tag)
+            plane = sbuf([P, PASS], U8, f"{name}_plane")
+            first = 0
+            for part in parts:
+                cols = slice(first, first + part.shape[1] // PACK)
+                nc.vector.quantize_mx(out=codes[:, cols].bitcast(FP8X4), scales=plane[:, cols], in_=part)
+                first = cols.stop
             return codes, plane
 
-        def gate(a, h, first, width):
-            if a + h + first == 0:
-                gated = keep.tile([P, PACK, width], F32, name="first_gated", tag="wu_raw0", align_bytes=64)
-            elif f"gated{a}_{h}" in PLACE:
-                gated = placed([P, PACK, width], F32, f"gated{a}_{h}")
-            else:
-                gated = work.tile([P, PACK, width], F32, name="gated", bufs=4)
-            tokens = slice(first, first + width)
-            if width == CHUNK:
-                one_bank = psum.tile([P, PACK, CHUNK], F32, name="wide_bank", bufs=4)
+        def wide_bank():
+            return psum.tile([P, HALF], F32, name="wide_bank", bufs=4)
+
+        def gate_pass(bank, a, h, t, first, width):
+            nc.tensor.matmul_mx(
+                out=bank,
+                lhsT=wg_codes[a].bitcast(U8)[:, 2 * P * t : 2 * P * (t + 1)].bitcast(FP4X4),
+                lhsT_scale=wg_planes[a][:, P * t : P * (t + 1)],
+                rhs=v_codes[h][:, first : first + width].bitcast(FP8X4),
+                rhs_scale=token_scales(h * HALF + first, width),
+                start=True,
+                stop=True,
+            )
+
+        def silu(gated, bank, a, t):
+            nc.scalar.activation(out=gated, in_=bank, func=SILU, bias=bias[:, a, t : t + 1])
+
+        def gate(a, h, first=0, tag=None, midway=None):
+            width = HALF - first
+            gated = sbuf([P, PACK, width], F32, f"gated{a}_{h}", tag)
             for t in range(PACK):
-                if width == CHUNK:
-                    bank = one_bank[:, t, :]
-                else:
-                    bank = psum.tile([P, HALF], F32, name="wide_bank", bufs=4)[:, :width]
-                nc.tensor.matmul_mx(
-                    out=bank,
-                    lhsT=wg_codes[a].bitcast(U8)[:, 2 * P * t : 2 * P * (t + 1)].bitcast(FP4X4),
-                    lhsT_scale=wg_planes[a][:, P * t : P * (t + 1)],
-                    rhs=v_codes[h][:, tokens].bitcast(FP8X4),
-                    rhs_scale=v_plane[:, h * HALF + first : h * HALF + first + width],
-                    start=True,
-                    stop=True,
-                )
-                if width > CHUNK:
-                    nc.scalar.activation(out=gated[:, t, :], in_=bank, func=SILU, bias=bias[:, a, t : t + 1])
-            if width == CHUNK:
-                for t in range(PACK):
-                    nc.scalar.activation(
-                        out=gated[:, t, :], in_=one_bank[:, t, :], func=SILU, bias=bias[:, a, t : t + 1]
-                    )
+                if midway and t == PACK // 2:
+                    midway()
+                bank = wide_bank()
+                cuts = (0, HALF) if first == 0 else (first, HALF // 2, HALF)
+                for lo, hi in zip(cuts, cuts[1:]):
+                    gate_pass(bank[:, lo - first : hi - first], a, h, t, lo, hi - lo)
+                silu(gated[:, t, :], bank[:, :width], a, t)
             return [gated[:, :, c : c + CHUNK] for c in range(0, width, CHUNK)]
 
-        def gates(a, h, pieces=slice(None)):
-            widths = GATE_WIDTHS.get((a, h), (HALF,))
-            starts = [(sum(widths[:k]), width) for k, width in enumerate(widths)]
-            return [chunk for first, width in starts[pieces] for chunk in gate(a, h, first, width)]
+        def gate_first_chunk(a, h):
+            gated = sbuf([P, PACK, CHUNK], F32, f"gated_first{a}_{h}")
+            bank = wide_bank()
+            for t in range(PACK):
+                gate_pass(bank[:, t * CHUNK : (t + 1) * CHUNK], a, h, t, 0, CHUNK)
+            for t in range(PACK):
+                silu(gated[:, t, :], bank[:, t * CHUNK : (t + 1) * CHUNK], a, t)
+            return [gated[:]]
 
         def up(a, h, c):
             bank = psum.tile([P, PACK, CHUNK], F32, name="up_bank", bufs=4)
@@ -199,17 +216,18 @@ def tile_list_paged_swiglu_residual_kernel(
                     lhsT=wu_mx[a][0][:, P * t : P * (t + 1)].bitcast(FP8X4),
                     lhsT_scale=wu_mx[a][1][:, P * t : P * (t + 1)],
                     rhs=v_codes[h][:, c * CHUNK : (c + 1) * CHUNK].bitcast(FP8X4),
-                    rhs_scale=v_plane[:, h * HALF + c * CHUNK : h * HALF + (c + 1) * CHUNK],
+                    rhs_scale=token_scales(h * HALF + c * CHUNK, CHUNK),
                     start=True,
                     stop=True,
                 )
             return bank
 
         def products(a, h, gated, first_chunk=0):
-            hidden = placed([P, HALF * PACK], BF16, f"hidden{a}_{h}")
-            for c in range(first_chunk, HALF // CHUNK):
+            hidden = sbuf([P, (CHUNKS - first_chunk) * PASS], BF16, f"hidden{a}_{h}")
+            for c in range(first_chunk, CHUNKS):
+                place = (c - first_chunk) * PASS
                 nc.vector.tensor_tensor(
-                    out=hidden[:, c * PASS : (c + 1) * PASS].rearrange("p (g i t) -> p g t i", i=RUN, t=PACK),
+                    out=hidden[:, place : place + PASS].rearrange("p (g i t) -> p g t i", i=RUN, t=PACK),
                     in0=up(a, h, c)[:].rearrange("p t (g i) -> p g t i", i=RUN),
                     in1=gated[c].rearrange("p t (g i) -> p g t i", i=RUN),
                     op=MULT,
@@ -217,12 +235,12 @@ def tile_list_paged_swiglu_residual_kernel(
             return hidden
 
         def copy_first_up(a, h):
-            copied = placed([P, CHUNK, PACK], F32, f"up_copied{a}")
+            copied = sbuf([P, CHUNK, PACK], F32, f"up_copied{a}")
             nc.scalar.copy(out=copied[:], in_=up(a, h, 0)[:].rearrange("p t c -> p c t"))
             return copied
 
         def product_on_gpsimd(a, copied, gated):
-            lead = placed([P, PASS], BF16, f"lead{a}")
+            lead = sbuf([P, PASS], BF16, f"lead{a}", "staged")
             nc.gpsimd.tensor_tensor(
                 out=lead[:].rearrange("p (c t) -> p c t", t=PACK),
                 in0=copied[:],
@@ -231,23 +249,23 @@ def tile_list_paged_swiglu_residual_kernel(
             )
             return lead
 
-        def down(n, h_mx):
-            bank = psum.tile([P, HALF], F32, name="wide_bank", bufs=4)
+        def down(h, n):
+            bank = wide_bank()
             for a in range(R_BLOCKS):
                 nc.tensor.matmul_mx(
                     out=bank[:],
                     lhsT=wd_codes[:, a, P * n : P * (n + 1)].bitcast(FP8X4),
                     lhsT_scale=wd_plane[:, a, :].bitcast(U8)[:, P * n : P * (n + 1)],
-                    rhs=h_mx[a][0][:].bitcast(FP8X4),
-                    rhs_scale=h_mx[a][1][:],
+                    rhs=h_mx[h][a][0][:].bitcast(FP8X4),
+                    rhs_scale=h_mx[h][a][1][:],
                     start=(a == 0),
                     stop=(a == R_BLOCKS - 1),
                 )
-            return bank
-
-        def finish(h, n):
             product = keep.tile([P, HALF], F32, name=f"product{h}_{n}")
-            nc.scalar.copy(out=product[:], in_=down(n, h_mx[h])[:])
+            nc.scalar.copy(out=product[:], in_=bank[:])
+            return product
+
+        def finish(h, n, product):
             result = keep.tile([P, HALF], F32, name=f"result{h}_{n}")
             cuts = (0, HALF - LAST_PIECE, HALF) if (h, n) == (1, N_TILES - 1) else (0, HALF)
             for first, end in zip(cuts, cuts[1:]):
@@ -257,68 +275,55 @@ def tile_list_paged_swiglu_residual_kernel(
                     out=out[n * P : (n + 1) * P, h * HALF + first : h * HALF + end], in_=result[:, first:end]
                 )
 
-        v_plane = keep.tile([P, S], U8, name="v_plane", align_bytes=64)
-        nc.vector.tensor_copy(v_plane[:], tab_plane[:].bitcast(U8).indirect(offsets[:]))
-        v_codes = [gather_words(0, "v_codes0")]
-        first_codes = keep.tile([P, PASS], U16, name="first_codes", align_bytes=64)
-        reorder(nc.vector, first_codes[:], first_words)
-        first_plane = keep.tile([P, PASS], U8, name="first_plane", align_bytes=64)
-        reorder(nc.vector, first_plane[:], wg_plane_first[:].bitcast(U8))
-        slots0, dst = slots_tile("wu_slots0", PACK)
-        nc.scalar.copy(out=dst[:, : P // 2], in_=wu_halves[0])
-        nc.vector.tensor_copy(out=dst[:, SCALAR_ROWS:], in_=wu_halves[1][:, SCALAR_ROWS - P // 2 :])
-        wu_mx = [quantize("wu0", "wu0", [slots0[:, t * PASS : (t + 1) * PASS] for t in range(PACK)], range(PACK))]
-        v_codes.append(gather_words(1, "wg_plane_first"))
-        later_codes = keep.tile([P, H - PASS], U16, name="later_codes", tag="wu_raw256", align_bytes=64)
-        reorder(nc.vector, later_codes[:], later_words)
+        first_codes = sbuf([P, PASS], U16, "first_codes")
+        nc.scalar.copy(**dealt(first_codes[:], first_raw[:].bitcast(U16)))
+        later_codes = sbuf([P, H - PASS], U16, "later_codes")
+        nc.scalar.copy(**dealt(later_codes[:], later_raw[:].bitcast(U16)))
         wg_codes = [first_codes[:], later_codes[:, :PASS], later_codes[:, PASS:]]
-        wg_planes = [first_plane[:]]
+        early_scales = gather_scales("early_scales", 0, EARLY_SCALES)
+        v_codes = [sbuf([P, HALF], U32, "v_codes0")]
+        gather_words(0, 0, HALF)
+        first_plane = deal_plane(0)
+        wg_planes = [first_plane, deal_plane(1)]
+        late_scales = gather_scales("late_scales", EARLY_SCALES, S)
+        slots = round_up_weight(0)
+        wu_mx = [quantize("wu0", [slots[:, : 2 * PASS], slots[:, 2 * PASS :]])]
+        wg_planes.append(deal_plane(2))
+        v_codes.append(sbuf([P, HALF], U32, "v_codes1"))
+        gather_words(1, 0, HALF)
         h_mx = ([], [])
 
-        def whole(a, h, hidden, tag=None):
-            h_mx[h].append(quantize(f"h{a}_{h}", tag or f"h{a}_{h}", [hidden[:]], (0,)))
+        gated = gate(0, 0, tag="wu_front0")
+        for a in range(R_BLOCKS - 1):
+            slots = round_up_weight(a + 1)
+            hidden = products(a, 0, gated)
+            wu_mx.append(quantize(f"wu{a + 1}", [slots[:]]))
+            h_mx[0].append(quantize(f"h{a}_0", [hidden[:]], f"wu_back{a + 1}"))
+            gated = gate(a + 1, 0, tag=f"wu_front{a + 1}")
 
-        slots1, dst1 = slots_tile("wu_slots1", PACK)
-        round_on_gpsimd(dst1[:, SECOND_SCALAR_ROWS:], wu_raw1[:, SECOND_SCALAR_ROWS:])
-        reorder_plane(1)
-        gated = [gates(0, 0), gates(0, 1)]
-        nc.scalar.copy(out=dst1[:, :SECOND_SCALAR_ROWS], in_=wu_raw1[:, :SECOND_SCALAR_ROWS])
-        whole(0, 0, products(0, 0, gated[0]))
+        copied = copy_first_up(0, 1)
+        second = gate_first_chunk(0, 1)
+        lead = product_on_gpsimd(0, copied, second)
+        second.extend(gate(0, 1, first=CHUNK))
+        h_mx[0].append(quantize("h2_0", [products(2, 0, gated)[:]]))
+        hidden = products(0, 1, second, first_chunk=1)
+        h_mx[1].append(quantize("h0_1", [lead[:], hidden[:]]))
 
-        early2, dst = slots_tile("wu_early2", 2, P // 2)
-        round_on_gpsimd(dst, last_halves[0][:, :, :, 2:])
-        hidden = products(0, 1, gated[1])
-        wu_mx.append(quantize("wu1", "wu1", [slots1[:]], (0,)))
-        whole(0, 1, hidden, f"wu_raw{PASS}")
-
-        reorder_plane(2)
-        upper2, dst = slots_tile("wu_upper2", PACK, P // 2)
-        round_on_gpsimd(dst, last_halves[1])
-        gated = [gates(1, 0)]
-        front2, dst = slots_tile("wu_front2", 2, P // 2)
-        nc.scalar.copy(out=dst, in_=last_halves[0][:, :, :, :2])
-        hidden = products(1, 0, gated[0])
         copied = copy_first_up(1, 1)
-        gated.append(gates(1, 1))
-        lower = [tile[:, t * 256 : (t + 1) * 256] for tile in (front2, early2) for t in range(2)]
-        parts = [part for t in range(PACK) for part in (lower[t], upper2[:, t * 256 : (t + 1) * 256])]
-        wu_mx.append(quantize("wu2", f"wu_raw{2 * PASS + PASS // 2}", parts, range(2 * PACK)))
-        whole(1, 0, hidden)
+        gated = gate(1, 1, midway=lambda: finish(0, 0, down(0, 0)))
+        lead = product_on_gpsimd(1, copied, gated)
+        hidden = products(1, 1, gated, first_chunk=1)
+        finish(0, 1, down(0, 1))
+        h_mx[1].append(quantize("h1_1", [lead[:], hidden[:]]))
 
-        def shared_unit(a, lead, hidden):
-            parts = [lead[:], hidden[:, PASS : 2 * PASS], hidden[:, 2 * PASS :]]
-            h_mx[1].append(quantize(f"h{a}_1", f"h{a}_1", parts, range(3)))
+        copied = copy_first_up(2, 1)
+        gated = gate(2, 1)
+        lead = product_on_gpsimd(2, copied, gated)
+        hidden = products(2, 1, gated, first_chunk=1)
+        waiting = [down(0, n) for n in (2, 3)]
+        finish(0, 2, waiting[0])
+        h_mx[1].append(quantize("h2_1", [lead[:], hidden[:]]))
+        finish(0, 3, waiting[1])
 
-        lead = product_on_gpsimd(1, copied, gated[1])
-        hidden = products(1, 1, gated[1], first_chunk=1)
-        gated = [gates(2, 0), gates(2, 1, slice(0, 1))]
-        shared_unit(1, lead, hidden)
-
-        lead = product_on_gpsimd(2, copy_first_up(2, 1), gated[1])
-        gated[1].extend(gates(2, 1, slice(1, None)))
-        whole(2, 0, products(2, 0, gated[0]))
-        shared_unit(2, lead, products(2, 1, gated[1], first_chunk=1))
-
-        for h in range(2):
-            for n in range(N_TILES):
-                finish(h, n)
+        for n in range(N_TILES):
+            finish(1, n, down(1, n))

@@ -23,25 +23,35 @@ PASS = P * PACK
 R_BLOCKS = H // PASS
 N_TILES = N // P
 HALF = S // 2
+QUARTER = S // 4
 CHUNK = 128
 CHUNKS = HALF // CHUNK
 RUN = 2
 LAST_PIECE = 128
-SCALAR_GROUPS = (64, 32, 32)
-EARLY_SCALES = HALF
+EARLY_SCALES = 768
 EARLY_COLUMNS = 640
 PLACE = {
-    "first_raw": 8192,
-    "late_scales": 8192,
-    "wu_back0": 10240,
-    "wg_plane2": 10240,
-    "v_codes1": 10752,
     "wu_slots0": 0,
-    "wu_slots1": 1024,
-    "wu_slots2": 1024,
-    "lead0": 1024,
-    "lead1": 1024,
-    "lead2": 1024,
+    "wu_slots1": 2048,
+    "wu_upper2": 2048,
+    "lead1": 2048,
+    "gated1_1_0": 4096,
+    "v_codes256": 16448,
+    "first_raw": 17408,
+    "late_scales": 17472,
+    "v_codes512": 17920,
+    "wu_raw256": 20480,
+    "wg_plane1": 20480,
+    "wg_plane2": 20992,
+    "hidden0_0": 28672,
+    "wu_lower2": 28672,
+    "hidden1_1": 32768,
+    "lead2": 32768,
+    "wu_raw0": 36864,
+    "gated0_0_0": 36864,
+    "wu_raw512": 45056,
+    "gated1_0_0": 45056,
+    "gated2_0_0": 45056,
 }
 
 
@@ -91,23 +101,15 @@ def tile_list_paged_swiglu_residual_kernel(
         later_raw = sbuf([P, (H - PASS) // 2], I32, "later_raw")
         nc.sync.dma_start(out=later_raw[:], in_=wg_words[0].bitcast(I32)[:, PASS // 2 :])
 
-        def load_up_weight(name, first, width):
-            raw = sbuf([P, PACK * width], F32, name)
+        def load_up_weight(first, width):
+            raw = sbuf([P, PACK * width], F32, f"wu_raw{first}")
             nc.sync.dma_start(
                 out=raw[:].rearrange("p (j c) -> p j c", j=PACK),
                 in_=wu[:, first : first + width].rearrange("(p j) c -> p j c", j=PACK),
             )
             return raw[:].rearrange("p (j m t) -> p m j t", j=PACK, t=PACK)
 
-        wu_raw = []
-        for a, groups in enumerate(SCALAR_GROUPS):
-            cut = PACK * groups
-            wu_raw.append(
-                (
-                    load_up_weight(f"wu_front{a}", a * PASS, cut),
-                    load_up_weight(f"wu_back{a}", a * PASS + cut, PASS - cut),
-                )
-            )
+        wu_halves = [load_up_weight(first, PASS // 2) for first in range(0, H, PASS // 2)]
         load_scale_rows(nc.sync, wd_plane, wd_scales.bitcast(I32).rearrange("a q c -> q a c"))
         wd_codes = sbuf([P, R_BLOCKS, N], I32, "wd_codes")
         nc.sync.dma_start(out=wd_codes[:], in_=wd_words.rearrange("a p c i -> p a (c i)").bitcast(I32))
@@ -120,9 +122,14 @@ def tile_list_paged_swiglu_residual_kernel(
         def listed(first, end):
             return offsets[:, first // 16 : end // 16]
 
-        def gather_words(h, first, end):
-            picked = tab_codes[:].bitcast(U32).indirect(listed(h * HALF + first, h * HALF + end))
-            nc.vector.tensor_copy(v_codes[h][:, first:end], picked)
+        def gather_words(first, end):
+            codes = sbuf([P, end - first], U32, f"v_codes{first}")
+            nc.vector.tensor_copy(codes[:], tab_codes[:].bitcast(U32).indirect(listed(first, end)))
+            v_codes[first] = codes
+
+        def token_codes(first, width):
+            start = max(key for key in v_codes if key <= first)
+            return v_codes[start][:, first - start : first - start + width].bitcast(FP8X4)
 
         def gather_scales(name, first, end):
             plane = sbuf([P, end - first], U8, name)
@@ -140,24 +147,23 @@ def tile_list_paged_swiglu_residual_kernel(
                 "in_": raw.rearrange("p (a m t) -> p a t m", t=PACK, m=P),
             }
 
+        def deal_words(a, raw):
+            codes = sbuf([P, PASS], U16, f"wg_codes{a}")
+            nc.scalar.copy(**dealt(codes[:], raw.bitcast(U16)))
+            return codes[:]
+
         def deal_plane(a):
             plane = sbuf([P, PASS], U8, f"wg_plane{a}")
             nc.vector.tensor_copy(**dealt(plane[:], wg_raw_plane[:].bitcast(U8)[:, a * PASS : (a + 1) * PASS]))
-            return plane[:]
+            wg_planes.append(plane[:])
 
-        def round_up_weight(a):
-            slots = sbuf([P, PASS * PACK], BF16, f"wu_slots{a}", "staged")
-            dst = slots[:].rearrange("p (t m j) -> p m j t", t=PACK, j=PACK)
-            cut = SCALAR_GROUPS[a]
-            front, back = wu_raw[a]
-            nc.scalar.copy(out=dst[:, :cut], in_=front)
-            if a == 0:
-                for pair in (slice(0, 2), slice(2, 4)):
-                    nc.vector.tensor_copy(out=dst[:, cut:, :, pair], in_=back[:, :, :, pair])
-            else:
-                walk = "p m j t -> p m t j"
-                nc.gpsimd.tensor_scalar(dst[:, cut:].rearrange(walk), back.rearrange(walk), 1.0, 0.0, MULT, ADD)
-            return slots
+        def slots_tile(name, groups):
+            tile = sbuf([P, PACK * groups * PACK], BF16, name)
+            return tile, tile[:].rearrange("p (t m j) -> p m j t", t=PACK, j=PACK)
+
+        def round_on_gpsimd(dst, src):
+            walk = "p m j t -> p m t j"
+            nc.gpsimd.tensor_scalar(dst.rearrange(walk), src.rearrange(walk), 1.0, 0.0, MULT, ADD)
 
         def quantize(name, parts, tag=None):
             codes = sbuf([P, PASS], U32, f"{name}_codes", tag)
@@ -177,7 +183,7 @@ def tile_list_paged_swiglu_residual_kernel(
                 out=bank,
                 lhsT=wg_codes[a].bitcast(U8)[:, 2 * P * t : 2 * P * (t + 1)].bitcast(FP4X4),
                 lhsT_scale=wg_planes[a][:, P * t : P * (t + 1)],
-                rhs=v_codes[h][:, first : first + width].bitcast(FP8X4),
+                rhs=token_codes(h * HALF + first, width),
                 rhs_scale=token_scales(h * HALF + first, width),
                 start=True,
                 stop=True,
@@ -186,27 +192,22 @@ def tile_list_paged_swiglu_residual_kernel(
         def silu(gated, bank, a, t):
             nc.scalar.activation(out=gated, in_=bank, func=SILU, bias=bias[:, a, t : t + 1])
 
-        def gate(a, h, first=0, tag=None, midway=None):
-            width = HALF - first
-            gated = sbuf([P, PACK, width], F32, f"gated{a}_{h}", tag)
-            for t in range(PACK):
-                if midway and t == PACK // 2:
-                    midway()
+        def gate(a, h, first=0, end=HALF):
+            width = end - first
+            gated = sbuf([P, PACK, width], F32, f"gated{a}_{h}_{first}")
+            if width == CHUNK:
                 bank = wide_bank()
-                cuts = (0, HALF) if first == 0 else (first, HALF // 2, HALF)
-                for lo, hi in zip(cuts, cuts[1:]):
-                    gate_pass(bank[:, lo - first : hi - first], a, h, t, lo, hi - lo)
-                silu(gated[:, t, :], bank[:, :width], a, t)
+                for t in range(PACK):
+                    gate_pass(bank[:, t * CHUNK : (t + 1) * CHUNK], a, h, t, first, CHUNK)
+                for t in range(PACK):
+                    silu(gated[:, t, :], bank[:, t * CHUNK : (t + 1) * CHUNK], a, t)
+            else:
+                for t in range(PACK):
+                    bank = wide_bank()
+                    for lo in range(first, end, QUARTER):
+                        gate_pass(bank[:, lo - first : lo - first + QUARTER], a, h, t, lo, QUARTER)
+                    silu(gated[:, t, :], bank[:, :width], a, t)
             return [gated[:, :, c : c + CHUNK] for c in range(0, width, CHUNK)]
-
-        def gate_first_chunk(a, h):
-            gated = sbuf([P, PACK, CHUNK], F32, f"gated_first{a}_{h}")
-            bank = wide_bank()
-            for t in range(PACK):
-                gate_pass(bank[:, t * CHUNK : (t + 1) * CHUNK], a, h, t, 0, CHUNK)
-            for t in range(PACK):
-                silu(gated[:, t, :], bank[:, t * CHUNK : (t + 1) * CHUNK], a, t)
-            return [gated[:]]
 
         def up(a, h, c):
             bank = psum.tile([P, PACK, CHUNK], F32, name="up_bank", bufs=4)
@@ -215,7 +216,7 @@ def tile_list_paged_swiglu_residual_kernel(
                     out=bank[:, t, :],
                     lhsT=wu_mx[a][0][:, P * t : P * (t + 1)].bitcast(FP8X4),
                     lhsT_scale=wu_mx[a][1][:, P * t : P * (t + 1)],
-                    rhs=v_codes[h][:, c * CHUNK : (c + 1) * CHUNK].bitcast(FP8X4),
+                    rhs=token_codes(h * HALF + c * CHUNK, CHUNK),
                     rhs_scale=token_scales(h * HALF + c * CHUNK, CHUNK),
                     start=True,
                     stop=True,
@@ -240,7 +241,7 @@ def tile_list_paged_swiglu_residual_kernel(
             return copied
 
         def product_on_gpsimd(a, copied, gated):
-            lead = sbuf([P, PASS], BF16, f"lead{a}", "staged")
+            lead = sbuf([P, PASS], BF16, f"lead{a}")
             nc.gpsimd.tensor_tensor(
                 out=lead[:].rearrange("p (c t) -> p c t", t=PACK),
                 in0=copied[:],
@@ -275,55 +276,63 @@ def tile_list_paged_swiglu_residual_kernel(
                     out=out[n * P : (n + 1) * P, h * HALF + first : h * HALF + end], in_=result[:, first:end]
                 )
 
-        first_codes = sbuf([P, PASS], U16, "first_codes")
-        nc.scalar.copy(**dealt(first_codes[:], first_raw[:].bitcast(U16)))
-        later_codes = sbuf([P, H - PASS], U16, "later_codes")
-        nc.scalar.copy(**dealt(later_codes[:], later_raw[:].bitcast(U16)))
-        wg_codes = [first_codes[:], later_codes[:, :PASS], later_codes[:, PASS:]]
+        wg_codes = [deal_words(0, first_raw[:])]
+        wg_codes.extend(deal_words(a, later_raw[:, (a - 1) * PASS // 2 : a * PASS // 2]) for a in (1, 2))
         early_scales = gather_scales("early_scales", 0, EARLY_SCALES)
-        v_codes = [sbuf([P, HALF], U32, "v_codes0")]
-        gather_words(0, 0, HALF)
-        first_plane = deal_plane(0)
-        wg_planes = [first_plane, deal_plane(1)]
+        v_codes = {}
+        gather_words(0, QUARTER)
+        wg_planes = []
+        deal_plane(0)
+        gather_words(QUARTER, HALF)
         late_scales = gather_scales("late_scales", EARLY_SCALES, S)
-        slots = round_up_weight(0)
+        gather_words(HALF, S)
+        slots, dst = slots_tile("wu_slots0", P)
+        nc.scalar.copy(out=dst[:, : P // 2], in_=wu_halves[0])
+        for pair in (slice(0, 2), slice(2, 4)):
+            nc.vector.tensor_copy(out=dst[:, P // 2 :, :, pair], in_=wu_halves[1][:, :, :, pair])
         wu_mx = [quantize("wu0", [slots[:, : 2 * PASS], slots[:, 2 * PASS :]])]
-        wg_planes.append(deal_plane(2))
-        v_codes.append(sbuf([P, HALF], U32, "v_codes1"))
-        gather_words(1, 0, HALF)
+        for a in (1, 2):
+            deal_plane(a)
         h_mx = ([], [])
 
-        gated = gate(0, 0, tag="wu_front0")
-        for a in range(R_BLOCKS - 1):
-            slots = round_up_weight(a + 1)
-            hidden = products(a, 0, gated)
-            wu_mx.append(quantize(f"wu{a + 1}", [slots[:]]))
-            h_mx[0].append(quantize(f"h{a}_0", [hidden[:]], f"wu_back{a + 1}"))
-            gated = gate(a + 1, 0, tag=f"wu_front{a + 1}")
+        def whole(a, h, hidden):
+            h_mx[h].append(quantize(f"h{a}_{h}", [hidden[:]]))
 
-        copied = copy_first_up(0, 1)
-        second = gate_first_chunk(0, 1)
-        lead = product_on_gpsimd(0, copied, second)
-        second.extend(gate(0, 1, first=CHUNK))
-        h_mx[0].append(quantize("h2_0", [products(2, 0, gated)[:]]))
-        hidden = products(0, 1, second, first_chunk=1)
-        h_mx[1].append(quantize("h0_1", [lead[:], hidden[:]]))
+        def shared_unit(a, lead, hidden):
+            h_mx[1].append(quantize(f"h{a}_1", [lead[:], hidden[:, :PASS], hidden[:, PASS:]]))
 
+        gated = [gate(0, 0), gate(0, 1)]
+        slots, dst = slots_tile("wu_slots1", P)
+        nc.scalar.copy(out=dst[:, : P // 2], in_=wu_halves[2])
+        round_on_gpsimd(dst[:, P // 2 :], wu_halves[3])
+        whole(0, 0, products(0, 0, gated[0]))
+
+        lower, dst = slots_tile("wu_lower2", P // 2)
+        round_on_gpsimd(dst, wu_halves[4])
+        hidden = products(0, 1, gated[1])
+        wu_mx.append(quantize("wu1", [slots[:]]))
+        whole(0, 1, hidden)
+
+        gated = [gate(1, 0)]
+        upper, dst = slots_tile("wu_upper2", P // 2)
+        round_on_gpsimd(dst, wu_halves[5])
+        gated.append(gate(1, 1))
+        hidden = products(1, 0, gated[0])
         copied = copy_first_up(1, 1)
-        gated = gate(1, 1, midway=lambda: finish(0, 0, down(0, 0)))
-        lead = product_on_gpsimd(1, copied, gated)
-        hidden = products(1, 1, gated, first_chunk=1)
-        finish(0, 1, down(0, 1))
-        h_mx[1].append(quantize("h1_1", [lead[:], hidden[:]]))
+        parts = [tile[:, t * 256 : (t + 1) * 256] for t in range(PACK) for tile in (lower, upper)]
+        wu_mx.append(quantize("wu2", parts, "wu_raw1280"))
+        whole(1, 0, hidden)
 
-        copied = copy_first_up(2, 1)
-        gated = gate(2, 1)
-        lead = product_on_gpsimd(2, copied, gated)
-        hidden = products(2, 1, gated, first_chunk=1)
-        waiting = [down(0, n) for n in (2, 3)]
-        finish(0, 2, waiting[0])
-        h_mx[1].append(quantize("h2_1", [lead[:], hidden[:]]))
-        finish(0, 3, waiting[1])
+        lead = product_on_gpsimd(1, copied, gated[1])
+        hidden = products(1, 1, gated[1], first_chunk=1)
+        gated = [gate(2, 0), gate(2, 1, 0, CHUNK)]
+        shared_unit(1, lead, hidden)
 
-        for n in range(N_TILES):
-            finish(1, n, down(1, n))
+        lead = product_on_gpsimd(2, copy_first_up(2, 1), gated[1])
+        gated[1].extend(gate(2, 1, CHUNK, QUARTER) + gate(2, 1, QUARTER, HALF))
+        whole(2, 0, products(2, 0, gated[0]))
+        shared_unit(2, lead, products(2, 1, gated[1], first_chunk=1))
+
+        for h in range(2):
+            for n in range(N_TILES):
+                finish(h, n, down(h, n))

@@ -28,8 +28,6 @@ CHUNK = 128
 CHUNKS = HALF // CHUNK
 RUN = 2
 LAST_PIECE = 128
-EARLY_SCALES = 768
-EARLY_COLUMNS = 640
 PLACE = {
     "wu_slots0": 0,
     "wu_slots1": 2048,
@@ -38,13 +36,10 @@ PLACE = {
     "gated1_1_0": 4096,
     "v_codes256": 16448,
     "first_raw": 17408,
-    "late_scales": 17472,
     "v_codes512": 17920,
     "wu_raw256": 20480,
-    "wg_plane1": 20480,
-    "wg_plane2": 20992,
-    "hidden0_0": 28672,
-    "wu_lower2": 28672,
+    "wg_planes1": 20480,
+    "wu_lower2": 0,
     "hidden1_1": 32768,
     "lead2": 32768,
     "wu_raw0": 36864,
@@ -75,11 +70,8 @@ def tile_list_paged_swiglu_residual_kernel(
                 return shared.tile(shape, dtype, name=name, align_bytes=64, offset=PLACE[name])
             return keep.tile(shape, dtype, name=name, tag=tag or name, align_bytes=64)
 
-        tab_codes = sbuf([P, T], I32, "tab_codes")
-        tab_rows = tab_words[0].rearrange("p t i -> p (t i)").bitcast(I32)
-        nc.sync.dma_start(out=tab_codes[:, :EARLY_COLUMNS], in_=tab_rows[:, :EARLY_COLUMNS])
-        bias = keep.tile([P, R_BLOCKS, PACK], F32, name="bias")
-        nc.sync.dma_start(out=bias[:], in_=bg.rearrange("(a p t) -> p a t", p=P, t=PACK))
+        later_raw = sbuf([P, (H - PASS) // 2], I32, "later_raw")
+        nc.sync.dma_start(out=later_raw[:], in_=wg_words[0].bitcast(I32)[:, PASS // 2 :])
         offsets = keep.tile([P, S // 16], U16, name="offsets")
         nc.sync.dma_start(offsets[:], offs)
 
@@ -94,12 +86,13 @@ def tile_list_paged_swiglu_residual_kernel(
         nc.scalar.activation(out=warm[:, 1:2], in_=warm[:, 0:1], func=SILU)
 
         load_scale_rows(nc.sync, tab_plane, tab_scales[0].bitcast(I32))
-        nc.sync.dma_start(out=tab_codes[:, EARLY_COLUMNS:], in_=tab_rows[:, EARLY_COLUMNS:])
+        tab_codes = sbuf([P, T], I32, "tab_codes")
+        nc.sync.dma_start(out=tab_codes[:], in_=tab_words[0].rearrange("p t i -> p (t i)").bitcast(I32))
         load_scale_rows(nc.sync, wg_raw_plane, wg_scales[0].bitcast(I32))
         first_raw = sbuf([P, PASS // 2], I32, "first_raw")
         nc.sync.dma_start(out=first_raw[:], in_=wg_words[0].bitcast(I32)[:, : PASS // 2])
-        later_raw = sbuf([P, (H - PASS) // 2], I32, "later_raw")
-        nc.sync.dma_start(out=later_raw[:], in_=wg_words[0].bitcast(I32)[:, PASS // 2 :])
+        bias = keep.tile([P, R_BLOCKS, PACK], F32, name="bias")
+        nc.sync.dma_start(out=bias[:], in_=bg.rearrange("(a p t) -> p a t", p=P, t=PACK))
 
         def load_up_weight(first, width):
             raw = sbuf([P, PACK * width], F32, f"wu_raw{first}")
@@ -131,15 +124,8 @@ def tile_list_paged_swiglu_residual_kernel(
             start = max(key for key in v_codes if key <= first)
             return v_codes[start][:, first - start : first - start + width].bitcast(FP8X4)
 
-        def gather_scales(name, first, end):
-            plane = sbuf([P, end - first], U8, name)
-            nc.vector.tensor_copy(plane[:], tab_plane[:].bitcast(U8).indirect(listed(first, end)))
-            return plane
-
         def token_scales(first, width):
-            if first < EARLY_SCALES:
-                return early_scales[:, first : first + width]
-            return late_scales[:, first - EARLY_SCALES : first - EARLY_SCALES + width]
+            return v_plane[:, first : first + width]
 
         def dealt(ordered, raw):
             return {
@@ -152,10 +138,10 @@ def tile_list_paged_swiglu_residual_kernel(
             nc.scalar.copy(**dealt(codes[:], raw.bitcast(U16)))
             return codes[:]
 
-        def deal_plane(a):
-            plane = sbuf([P, PASS], U8, f"wg_plane{a}")
-            nc.vector.tensor_copy(**dealt(plane[:], wg_raw_plane[:].bitcast(U8)[:, a * PASS : (a + 1) * PASS]))
-            wg_planes.append(plane[:])
+        def deal_planes(first, end):
+            planes = sbuf([P, (end - first) * PASS], U8, f"wg_planes{first}")
+            nc.vector.tensor_copy(**dealt(planes[:], wg_raw_plane[:].bitcast(U8)[:, first * PASS : end * PASS]))
+            wg_planes.extend(planes[:, k * PASS : (k + 1) * PASS] for k in range(end - first))
 
         def slots_tile(name, groups):
             tile = sbuf([P, PACK * groups * PACK], BF16, name)
@@ -278,25 +264,24 @@ def tile_list_paged_swiglu_residual_kernel(
 
         wg_codes = [deal_words(0, first_raw[:])]
         wg_codes.extend(deal_words(a, later_raw[:, (a - 1) * PASS // 2 : a * PASS // 2]) for a in (1, 2))
-        early_scales = gather_scales("early_scales", 0, EARLY_SCALES)
+        v_plane = sbuf([P, S], U8, "v_plane")
+        nc.vector.tensor_copy(v_plane[:], tab_plane[:].bitcast(U8).indirect(offsets[:]))
         v_codes = {}
         gather_words(0, QUARTER)
         wg_planes = []
-        deal_plane(0)
+        deal_planes(0, 1)
         gather_words(QUARTER, HALF)
-        late_scales = gather_scales("late_scales", EARLY_SCALES, S)
         gather_words(HALF, S)
         slots, dst = slots_tile("wu_slots0", P)
         nc.scalar.copy(out=dst[:, : P // 2], in_=wu_halves[0])
         for pair in (slice(0, 2), slice(2, 4)):
             nc.vector.tensor_copy(out=dst[:, P // 2 :, :, pair], in_=wu_halves[1][:, :, :, pair])
         wu_mx = [quantize("wu0", [slots[:, : 2 * PASS], slots[:, 2 * PASS :]])]
-        for a in (1, 2):
-            deal_plane(a)
+        deal_planes(1, R_BLOCKS)
         h_mx = ([], [])
 
-        def whole(a, h, hidden):
-            h_mx[h].append(quantize(f"h{a}_{h}", [hidden[:]]))
+        def whole(a, h, hidden, tag=None):
+            h_mx[h].append(quantize(f"h{a}_{h}", [hidden[:]], tag))
 
         def shared_unit(a, lead, hidden):
             h_mx[1].append(quantize(f"h{a}_1", [lead[:], hidden[:, :PASS], hidden[:, PASS:]]))
@@ -305,13 +290,12 @@ def tile_list_paged_swiglu_residual_kernel(
         slots, dst = slots_tile("wu_slots1", P)
         nc.scalar.copy(out=dst[:, : P // 2], in_=wu_halves[2])
         round_on_gpsimd(dst[:, P // 2 :], wu_halves[3])
-        whole(0, 0, products(0, 0, gated[0]))
-
         lower, dst = slots_tile("wu_lower2", P // 2)
         round_on_gpsimd(dst, wu_halves[4])
-        hidden = products(0, 1, gated[1])
+        hidden = [products(0, h, gated[h]) for h in range(2)]
+        whole(0, 0, hidden[0], "wu_raw1024")
         wu_mx.append(quantize("wu1", [slots[:]]))
-        whole(0, 1, hidden)
+        whole(0, 1, hidden[1])
 
         gated = [gate(1, 0)]
         upper, dst = slots_tile("wu_upper2", P // 2)

@@ -28,25 +28,36 @@ CHUNK = 128
 CHUNKS = HALF // CHUNK
 RUN = 2
 LAST_PIECE = 128
+SCALAR_GROUPS = 56
+EARLY_SCALES = 768
+EARLY_COLUMNS = 512
 PLACE = {
+    "late_scales": 17472,
+    "later_codes": 21504,
     "wu_slots0": 0,
-    "wu_slots1": 2048,
-    "wu_upper2": 2048,
-    "lead1": 2048,
-    "gated1_1_0": 4096,
+    "wg_plane1": 2048,
+    "wu_slots1": 2560,
+    "hidden0_0": 57344,
+    "wg_plane2": 57344,
+    "wu_upper2": 57856,
+    "lead1": 57856,
+    "gated1_1_0": 5120,
     "v_codes256": 16448,
     "first_raw": 17408,
     "v_codes512": 17920,
-    "wu_raw256": 20480,
-    "wg_planes1": 20480,
     "wu_lower2": 0,
-    "hidden1_1": 32768,
-    "lead2": 32768,
+    "wu_raw224": 20480,
+    "hidden1_1": 0,
+    "lead2": 0,
+    "wu2_codes": 28672,
+    "wu_raw1280": 29696,
+    "h1_0_codes": 30720,
     "wu_raw0": 36864,
     "gated0_0_0": 36864,
-    "wu_raw512": 45056,
-    "gated1_0_0": 45056,
-    "gated2_0_0": 45056,
+    "wu_raw768": 45056,
+    "h0_0_codes": 45056,
+    "gated1_0_0": 47104,
+    "gated2_0_0": 47104,
 }
 
 
@@ -70,15 +81,18 @@ def tile_list_paged_swiglu_residual_kernel(
                 return shared.tile(shape, dtype, name=name, align_bytes=64, offset=PLACE[name])
             return keep.tile(shape, dtype, name=name, tag=tag or name, align_bytes=64)
 
-        later_raw = sbuf([P, (H - PASS) // 2], I32, "later_raw")
-        nc.sync.dma_start(out=later_raw[:], in_=wg_words[0].bitcast(I32)[:, PASS // 2 :])
+        tab_codes = sbuf([P, T], I32, "tab_codes")
+        tab_rows = tab_words[0].rearrange("p t i -> p (t i)").bitcast(I32)
+        nc.sync.dma_start(out=tab_codes[:, :EARLY_COLUMNS], in_=tab_rows[:, :EARLY_COLUMNS])
         offsets = keep.tile([P, S // 16], U16, name="offsets")
         nc.sync.dma_start(offsets[:], offs)
 
         tab_plane = sbuf([P, T // 4], I32, "tab_plane")
         nc.vector.memset(tab_plane[:], 0)
-        wg_raw_plane = sbuf([P, H // 4], I32, "wg_raw_plane")
-        nc.vector.memset(wg_raw_plane[:], 0)
+        first_rows = sbuf([P, PASS // 4], I32, "first_rows")
+        nc.vector.memset(first_rows[:], 0)
+        later_rows = sbuf([P, (H - PASS) // 4], I32, "later_rows")
+        nc.vector.memset(later_rows[:], 0)
         wd_plane = sbuf([P, R_BLOCKS, N // 4], I32, "wd_plane")
         nc.vector.memset(wd_plane[:], 0)
         warm = keep.tile([P, 2], F32, name="warm")
@@ -86,13 +100,10 @@ def tile_list_paged_swiglu_residual_kernel(
         nc.scalar.activation(out=warm[:, 1:2], in_=warm[:, 0:1], func=SILU)
 
         load_scale_rows(nc.sync, tab_plane, tab_scales[0].bitcast(I32))
-        tab_codes = sbuf([P, T], I32, "tab_codes")
-        nc.sync.dma_start(out=tab_codes[:], in_=tab_words[0].rearrange("p t i -> p (t i)").bitcast(I32))
-        load_scale_rows(nc.sync, wg_raw_plane, wg_scales[0].bitcast(I32))
+        nc.sync.dma_start(out=tab_codes[:, EARLY_COLUMNS:], in_=tab_rows[:, EARLY_COLUMNS:])
+        load_scale_rows(nc.sync, first_rows, wg_scales[0].bitcast(I32)[:, : PASS // 4])
         first_raw = sbuf([P, PASS // 2], I32, "first_raw")
         nc.sync.dma_start(out=first_raw[:], in_=wg_words[0].bitcast(I32)[:, : PASS // 2])
-        bias = keep.tile([P, R_BLOCKS, PACK], F32, name="bias")
-        nc.sync.dma_start(out=bias[:], in_=bg.rearrange("(a p t) -> p a t", p=P, t=PACK))
 
         def load_up_weight(first, width):
             raw = sbuf([P, PACK * width], F32, f"wu_raw{first}")
@@ -102,7 +113,16 @@ def tile_list_paged_swiglu_residual_kernel(
             )
             return raw[:].rearrange("p (j m t) -> p m j t", j=PACK, t=PACK)
 
-        wu_halves = [load_up_weight(first, PASS // 2) for first in range(0, H, PASS // 2)]
+        cut = PACK * SCALAR_GROUPS
+        wu_halves = [load_up_weight(0, cut)]
+        bias = keep.tile([P, R_BLOCKS, PACK], F32, name="bias")
+        nc.sync.dma_start(out=bias[:], in_=bg.rearrange("(a p t) -> p a t", p=P, t=PACK))
+        wu_halves.append(load_up_weight(cut, PASS - cut))
+        later_raw = sbuf([P, (H - PASS) // 2], I32, "later_raw")
+        nc.sync.dma_start(out=later_raw[:], in_=wg_words[0].bitcast(I32)[:, PASS // 2 :])
+        wu_halves.append(load_up_weight(PASS, PASS // 2))
+        load_scale_rows(nc.sync, later_rows, wg_scales[0].bitcast(I32)[:, PASS // 4 :])
+        wu_halves.extend(load_up_weight(first, PASS // 2) for first in range(PASS + PASS // 2, H, PASS // 2))
         load_scale_rows(nc.sync, wd_plane, wd_scales.bitcast(I32).rearrange("a q c -> q a c"))
         wd_codes = sbuf([P, R_BLOCKS, N], I32, "wd_codes")
         nc.sync.dma_start(out=wd_codes[:], in_=wd_words.rearrange("a p c i -> p a (c i)").bitcast(I32))
@@ -124,8 +144,15 @@ def tile_list_paged_swiglu_residual_kernel(
             start = max(key for key in v_codes if key <= first)
             return v_codes[start][:, first - start : first - start + width].bitcast(FP8X4)
 
+        def gather_scales(name, first, end):
+            plane = sbuf([P, end - first], U8, name)
+            nc.vector.tensor_copy(plane[:], tab_plane[:].bitcast(U8).indirect(listed(first, end)))
+            return plane
+
         def token_scales(first, width):
-            return v_plane[:, first : first + width]
+            if first < EARLY_SCALES:
+                return early_scales[:, first : first + width]
+            return late_scales[:, first - EARLY_SCALES : first - EARLY_SCALES + width]
 
         def dealt(ordered, raw):
             return {
@@ -138,10 +165,10 @@ def tile_list_paged_swiglu_residual_kernel(
             nc.scalar.copy(**dealt(codes[:], raw.bitcast(U16)))
             return codes[:]
 
-        def deal_planes(first, end):
-            planes = sbuf([P, (end - first) * PASS], U8, f"wg_planes{first}")
-            nc.vector.tensor_copy(**dealt(planes[:], wg_raw_plane[:].bitcast(U8)[:, first * PASS : end * PASS]))
-            wg_planes.extend(planes[:, k * PASS : (k + 1) * PASS] for k in range(end - first))
+        def deal_plane(engine, a, rows):
+            plane = sbuf([P, PASS], U8, f"wg_plane{a}")
+            engine.tensor_copy(**dealt(plane[:], rows.bitcast(U8)))
+            wg_planes.append(plane[:])
 
         def slots_tile(name, groups):
             tile = sbuf([P, PACK * groups * PACK], BF16, name)
@@ -263,21 +290,22 @@ def tile_list_paged_swiglu_residual_kernel(
                 )
 
         wg_codes = [deal_words(0, first_raw[:])]
-        wg_codes.extend(deal_words(a, later_raw[:, (a - 1) * PASS // 2 : a * PASS // 2]) for a in (1, 2))
-        v_plane = sbuf([P, S], U8, "v_plane")
-        nc.vector.tensor_copy(v_plane[:], tab_plane[:].bitcast(U8).indirect(offsets[:]))
+        early_scales = gather_scales("early_scales", 0, EARLY_SCALES)
         v_codes = {}
         gather_words(0, QUARTER)
         wg_planes = []
-        deal_planes(0, 1)
+        deal_plane(nc.vector, 0, first_rows[:])
         gather_words(QUARTER, HALF)
+        late_scales = gather_scales("late_scales", EARLY_SCALES, S)
         gather_words(HALF, S)
         slots, dst = slots_tile("wu_slots0", P)
-        nc.scalar.copy(out=dst[:, : P // 2], in_=wu_halves[0])
+        nc.scalar.copy(out=dst[:, :SCALAR_GROUPS], in_=wu_halves[0])
         for pair in (slice(0, 2), slice(2, 4)):
-            nc.vector.tensor_copy(out=dst[:, P // 2 :, :, pair], in_=wu_halves[1][:, :, :, pair])
+            nc.vector.tensor_copy(out=dst[:, SCALAR_GROUPS:, :, pair], in_=wu_halves[1][:, :, :, pair])
         wu_mx = [quantize("wu0", [slots[:, : 2 * PASS], slots[:, 2 * PASS :]])]
-        deal_planes(1, R_BLOCKS)
+        later_codes = sbuf([P, H - PASS], U16, "later_codes")
+        nc.vector.tensor_copy(**dealt(later_codes[:], later_raw[:].bitcast(U16)))
+        wg_codes.extend([later_codes[:, :PASS], later_codes[:, PASS:]])
         h_mx = ([], [])
 
         def whole(a, h, hidden, tag=None):
@@ -288,23 +316,25 @@ def tile_list_paged_swiglu_residual_kernel(
 
         gated = [gate(0, 0), gate(0, 1)]
         slots, dst = slots_tile("wu_slots1", P)
-        nc.scalar.copy(out=dst[:, : P // 2], in_=wu_halves[2])
-        round_on_gpsimd(dst[:, P // 2 :], wu_halves[3])
+        round_on_gpsimd(dst[:, : P // 2], wu_halves[2])
+        nc.scalar.copy(out=dst[:, P // 2 :], in_=wu_halves[3])
+        deal_plane(nc.gpsimd, 1, later_rows[:, : PASS // 4])
         lower, dst = slots_tile("wu_lower2", P // 2)
         round_on_gpsimd(dst, wu_halves[4])
         hidden = [products(0, h, gated[h]) for h in range(2)]
-        whole(0, 0, hidden[0], "wu_raw1024")
         wu_mx.append(quantize("wu1", [slots[:]]))
-        whole(0, 1, hidden[1])
+        whole(0, 0, hidden[0])
+        whole(0, 1, hidden[1], "wu_raw1024")
 
         gated = [gate(1, 0)]
+        deal_plane(nc.gpsimd, 2, later_rows[:, PASS // 4 :])
         upper, dst = slots_tile("wu_upper2", P // 2)
         round_on_gpsimd(dst, wu_halves[5])
         gated.append(gate(1, 1))
         hidden = products(1, 0, gated[0])
         copied = copy_first_up(1, 1)
         parts = [tile[:, t * 256 : (t + 1) * 256] for t in range(PACK) for tile in (lower, upper)]
-        wu_mx.append(quantize("wu2", parts, "wu_raw1280"))
+        wu_mx.append(quantize("wu2", parts))
         whole(1, 0, hidden)
 
         lead = product_on_gpsimd(1, copied, gated[1])

@@ -28,7 +28,7 @@ CHUNK = 128
 CHUNKS = HALF // CHUNK
 RUN = 2
 LAST_PIECE = 128
-SCALAR_GROUPS = 56
+SCALAR_GROUPS = 48
 EARLY_SCALES = 768
 EARLY_COLUMNS = 512
 PLACE = {
@@ -46,7 +46,7 @@ PLACE = {
     "first_raw": 17408,
     "v_codes512": 17920,
     "wu_lower2": 0,
-    "wu_raw224": 20480,
+    "wu_raw192": 20480,
     "hidden1_1": 0,
     "lead2": 0,
     "wu2_codes": 28672,
@@ -105,22 +105,32 @@ def tile_list_paged_swiglu_residual_kernel(
         first_raw = sbuf([P, PASS // 2], I32, "first_raw")
         nc.sync.dma_start(out=first_raw[:], in_=wg_words[0].bitcast(I32)[:, : PASS // 2])
 
-        def load_up_weight(first, width):
+        def load_up_weight(first, width, midway=None):
             raw = sbuf([P, PACK * width], F32, f"wu_raw{first}")
-            nc.sync.dma_start(
-                out=raw[:].rearrange("p (j c) -> p j c", j=PACK),
-                in_=wu[:, first : first + width].rearrange("(p j) c -> p j c", j=PACK),
-            )
+            dst = raw[:].rearrange("p (j c) -> p j c", j=PACK)
+            src = wu[:, first : first + width].rearrange("(p j) c -> p j c", j=PACK)
+            if midway:
+                nc.sync.dma_start(out=dst[:, :2], in_=src[:, :2])
+                midway()
+                nc.sync.dma_start(out=dst[:, 2:], in_=src[:, 2:])
+            else:
+                nc.sync.dma_start(out=dst, in_=src)
             return raw[:].rearrange("p (j m t) -> p m j t", j=PACK, t=PACK)
+
+        def load_bias(first, end):
+            tile = keep.tile([P, end - first, PACK], F32, name=f"bias{first}")
+            rows = bg.rearrange("(a p t) -> p a t", p=P, t=PACK)
+            nc.sync.dma_start(out=tile[:], in_=rows[:, first:end, :])
+            return tile
 
         cut = PACK * SCALAR_GROUPS
         wu_halves = [load_up_weight(0, cut)]
-        bias = keep.tile([P, R_BLOCKS, PACK], F32, name="bias")
-        nc.sync.dma_start(out=bias[:], in_=bg.rearrange("(a p t) -> p a t", p=P, t=PACK))
-        wu_halves.append(load_up_weight(cut, PASS - cut))
+        biases = []
+        wu_halves.append(load_up_weight(cut, PASS - cut, midway=lambda: biases.append(load_bias(0, 1))))
         later_raw = sbuf([P, (H - PASS) // 2], I32, "later_raw")
         nc.sync.dma_start(out=later_raw[:], in_=wg_words[0].bitcast(I32)[:, PASS // 2 :])
         wu_halves.append(load_up_weight(PASS, PASS // 2))
+        biases.append(load_bias(1, R_BLOCKS))
         load_scale_rows(nc.sync, later_rows, wg_scales[0].bitcast(I32)[:, PASS // 4 :])
         wu_halves.extend(load_up_weight(first, PASS // 2) for first in range(PASS + PASS // 2, H, PASS // 2))
         load_scale_rows(nc.sync, wd_plane, wd_scales.bitcast(I32).rearrange("a q c -> q a c"))
@@ -188,8 +198,8 @@ def tile_list_paged_swiglu_residual_kernel(
                 first = cols.stop
             return codes, plane
 
-        def wide_bank():
-            return psum.tile([P, HALF], F32, name="wide_bank", bufs=4)
+        def wide_bank(name="wide_bank"):
+            return psum.tile([P, HALF], F32, name=name, bufs=4)
 
         def gate_pass(bank, a, h, t, first, width):
             nc.tensor.matmul_mx(
@@ -203,7 +213,7 @@ def tile_list_paged_swiglu_residual_kernel(
             )
 
         def silu(gated, bank, a, t):
-            nc.scalar.activation(out=gated, in_=bank, func=SILU, bias=bias[:, a, t : t + 1])
+            nc.scalar.activation(out=gated, in_=bank, func=SILU, bias=biases[min(a, 1)][:, max(a - 1, 0), t : t + 1])
 
         def gate(a, h, first=0, end=HALF):
             width = end - first
@@ -216,8 +226,9 @@ def tile_list_paged_swiglu_residual_kernel(
                     silu(gated[:, t, :], bank[:, t * CHUNK : (t + 1) * CHUNK], a, t)
             else:
                 for t in range(PACK):
-                    bank = wide_bank()
-                    for lo in range(first, end, QUARTER):
+                    bank = wide_bank("up_bank" if (a, h, t) == (0, 1, 0) else "wide_bank")
+                    starts = list(range(first, end, QUARTER))
+                    for lo in starts if t < PACK // 2 else reversed(starts):
                         gate_pass(bank[:, lo - first : lo - first + QUARTER], a, h, t, lo, QUARTER)
                     silu(gated[:, t, :], bank[:, :width], a, t)
             return [gated[:, :, c : c + CHUNK] for c in range(0, width, CHUNK)]

@@ -29,6 +29,7 @@ CHUNKS = HALF // CHUNK
 RUN = 2
 LAST_PIECE = 128
 SCALAR_GROUPS = 48
+GPSIMD_GROUPS = 40
 EARLY_SCALES = 768
 EARLY_COLUMNS = 512
 PLACE = {
@@ -46,7 +47,7 @@ PLACE = {
     "first_raw": 17408,
     "v_codes512": 17920,
     "wu_lower2": 0,
-    "wu_raw192": 20480,
+    "wu_raw352": 20480,
     "hidden1_1": 0,
     "lead2": 0,
     "wu2_codes": 28672,
@@ -105,16 +106,12 @@ def tile_list_paged_swiglu_residual_kernel(
         first_raw = sbuf([P, PASS // 2], I32, "first_raw")
         nc.sync.dma_start(out=first_raw[:], in_=wg_words[0].bitcast(I32)[:, : PASS // 2])
 
-        def load_up_weight(first, width, midway=None):
+        def load_up_weight(first, width):
             raw = sbuf([P, PACK * width], F32, f"wu_raw{first}")
-            dst = raw[:].rearrange("p (j c) -> p j c", j=PACK)
-            src = wu[:, first : first + width].rearrange("(p j) c -> p j c", j=PACK)
-            if midway:
-                nc.sync.dma_start(out=dst[:, :2], in_=src[:, :2])
-                midway()
-                nc.sync.dma_start(out=dst[:, 2:], in_=src[:, 2:])
-            else:
-                nc.sync.dma_start(out=dst, in_=src)
+            nc.sync.dma_start(
+                out=raw[:].rearrange("p (j c) -> p j c", j=PACK),
+                in_=wu[:, first : first + width].rearrange("(p j) c -> p j c", j=PACK),
+            )
             return raw[:].rearrange("p (j m t) -> p m j t", j=PACK, t=PACK)
 
         def load_bias(first, end):
@@ -125,8 +122,10 @@ def tile_list_paged_swiglu_residual_kernel(
 
         cut = PACK * SCALAR_GROUPS
         wu_halves = [load_up_weight(0, cut)]
-        biases = []
-        wu_halves.append(load_up_weight(cut, PASS - cut, midway=lambda: biases.append(load_bias(0, 1))))
+        middle = load_up_weight(cut, PACK * GPSIMD_GROUPS)
+        biases = [load_bias(0, 1)]
+        cut = cut + PACK * GPSIMD_GROUPS
+        wu_halves.append(load_up_weight(cut, PASS - cut))
         later_raw = sbuf([P, (H - PASS) // 2], I32, "later_raw")
         nc.sync.dma_start(out=later_raw[:], in_=wg_words[0].bitcast(I32)[:, PASS // 2 :])
         wu_halves.append(load_up_weight(PASS, PASS // 2))
@@ -311,8 +310,10 @@ def tile_list_paged_swiglu_residual_kernel(
         gather_words(HALF, S)
         slots, dst = slots_tile("wu_slots0", P)
         nc.scalar.copy(out=dst[:, :SCALAR_GROUPS], in_=wu_halves[0])
+        rest = SCALAR_GROUPS + GPSIMD_GROUPS
+        round_on_gpsimd(dst[:, SCALAR_GROUPS:rest], middle)
         for pair in (slice(0, 2), slice(2, 4)):
-            nc.vector.tensor_copy(out=dst[:, SCALAR_GROUPS:, :, pair], in_=wu_halves[1][:, :, :, pair])
+            nc.vector.tensor_copy(out=dst[:, rest:, :, pair], in_=wu_halves[1][:, :, :, pair])
         wu_mx = [quantize("wu0", [slots[:, : 2 * PASS], slots[:, 2 * PASS :]])]
         later_codes = sbuf([P, H - PASS], U16, "later_codes")
         nc.vector.tensor_copy(**dealt(later_codes[:], later_raw[:].bitcast(U16)))

@@ -29,6 +29,7 @@ CHUNKS = HALF // CHUNK
 RUN = 2
 LAST_PIECE = 128
 SCALAR_GROUPS = 48
+SCALAR_SHARE = 24
 GPSIMD_GROUPS = 40
 EARLY_SCALES = 768
 EARLY_COLUMNS = 512
@@ -48,6 +49,7 @@ PLACE = {
     "v_codes512": 17920,
     "wu_lower2": 0,
     "wu_raw352": 20480,
+    "wu_raw192": 23040,
     "hidden1_1": 0,
     "lead2": 0,
     "wu2_codes": 28672,
@@ -121,9 +123,9 @@ def tile_list_paged_swiglu_residual_kernel(
             return tile
 
         cut = PACK * SCALAR_GROUPS
+        biases = [load_bias(0, 1)]
         wu_halves = [load_up_weight(0, cut)]
         middle = load_up_weight(cut, PACK * GPSIMD_GROUPS)
-        biases = [load_bias(0, 1)]
         cut = cut + PACK * GPSIMD_GROUPS
         wu_halves.append(load_up_weight(cut, PASS - cut))
         later_raw = sbuf([P, (H - PASS) // 2], I32, "later_raw")
@@ -225,6 +227,12 @@ def tile_list_paged_swiglu_residual_kernel(
                     silu(gated[:, t, :], bank[:, t * CHUNK : (t + 1) * CHUNK], a, t)
             else:
                 for t in range(PACK):
+                    if (a, h) == (0, 0) and t < PACK // 2:
+                        for lo, name in ((0, "wide_bank"), (QUARTER, "up_bank")):
+                            bank = wide_bank(name)
+                            gate_pass(bank[:, :QUARTER], a, h, t, lo, QUARTER)
+                            silu(gated[:, t, lo : lo + QUARTER], bank[:, :QUARTER], a, t)
+                        continue
                     bank = wide_bank("up_bank" if (a, h, t) == (0, 1, 0) else "wide_bank")
                     starts = list(range(first, end, QUARTER))
                     for lo in starts if t < PACK // 2 else reversed(starts):
@@ -234,7 +242,7 @@ def tile_list_paged_swiglu_residual_kernel(
 
         def up(a, h, c):
             bank = psum.tile([P, PACK, CHUNK], F32, name="up_bank", bufs=4)
-            for t in range(PACK):
+            for t in range(PACK) if c == 0 else reversed(range(PACK)):
                 nc.tensor.matmul_mx(
                     out=bank[:, t, :],
                     lhsT=wu_mx[a][0][:, P * t : P * (t + 1)].bitcast(FP8X4),
@@ -309,7 +317,8 @@ def tile_list_paged_swiglu_residual_kernel(
         late_scales = gather_scales("late_scales", EARLY_SCALES, S)
         gather_words(HALF, S)
         slots, dst = slots_tile("wu_slots0", P)
-        nc.scalar.copy(out=dst[:, :SCALAR_GROUPS], in_=wu_halves[0])
+        nc.scalar.copy(out=dst[:, :SCALAR_SHARE], in_=wu_halves[0][:, :SCALAR_SHARE])
+        round_on_gpsimd(dst[:, SCALAR_SHARE:SCALAR_GROUPS], wu_halves[0][:, SCALAR_SHARE:])
         rest = SCALAR_GROUPS + GPSIMD_GROUPS
         round_on_gpsimd(dst[:, SCALAR_GROUPS:rest], middle)
         for pair in (slice(0, 2), slice(2, 4)):

from contextlib import ExitStack

import concourse.mybir as mybir

K, H, N, T, S = 512, 1536, 512, 2048, 1024
FLOPS = 2 * S * H * (2 * K + N)

F32 = mybir.dt.float32
BF16 = mybir.dt.bfloat16
I32 = mybir.dt.int32
U32 = mybir.dt.uint32
U16 = mybir.dt.uint16
U8 = mybir.dt.uint8
FP8X4 = mybir.dt.float8_e4m3fn_x4
FP4X4 = mybir.dt.float4_e2m1fn_x4
ADD = mybir.AluOpType.add
MULT = mybir.AluOpType.mult
SILU = mybir.ActivationFunctionType.Silu

P = 128
PACK = 4
PASS = P * PACK
R_BLOCKS = H // PASS
N_TILES = N // P
HALF = S // 2
QUARTER = S // 4
CHUNK = 128
CHUNKS = HALF // CHUNK
RUN = 2
LAST_PIECE = 128
SCALAR_GROUPS = 48
SCALAR_SHARE = 24
GPSIMD_GROUPS = 40
EARLY_SCALES = 768
EARLY_COLUMNS = 512
PLACE = {
    "late_scales": 17472,
    "later_codes": 21504,
    "wu_slots0": 0,
    "wg_plane1": 2048,
    "wu_slots1": 2560,
    "hidden0_0": 57344,
    "wg_plane2": 57344,
    "wu_upper2": 57856,
    "lead1": 57856,
    "gated1_1_0": 5120,
    "v_codes256": 16448,
    "first_raw": 17408,
    "v_codes512": 17920,
    "wu_lower2": 0,
    "wu_raw352": 20480,
    "wu_raw192": 23040,
    "hidden1_1": 0,
    "lead2": 0,
    "wu2_codes": 28672,
    "wu_raw1280": 29696,
    "h1_0_codes": 30720,
    "wu_raw0": 36864,
    "gated0_0_0": 36864,
    "wu_raw768": 45056,
    "h0_0_codes": 45056,
    "gated1_0_0": 47104,
    "gated2_0_0": 47104,
}


def load_scale_rows(queue, plane, rows):
    for q in range(4):
        queue.dma_start(out=plane[32 * q : 32 * q + 4], in_=rows[4 * q : 4 * q + 4])


def tile_list_paged_swiglu_residual_kernel(
    tc, tab_words, tab_scales, offs, wg_words, wg_scales, wu, wd_words, wd_scales, bg, gT, out
):
    nc = tc.nc
    with ExitStack() as ctx:
        keep = ctx.enter_context(tc.tile_pool(name="keep", bufs=1))
        psum = ctx.enter_context(tc.psum_pool(name="psum", bufs=1))

        shared = ctx.enter_context(tc.tile_pool(name="shared", bufs=1))

        def sbuf(shape, dtype, name, tag=None):
            if name in PLACE:
                return shared.tile(shape, dtype, name=name, align_bytes=64, offset=PLACE[name])
            return keep.tile(shape, dtype, name=name, tag=tag or name, align_bytes=64)

        tab_codes = sbuf([P, T], I32, "tab_codes")
        tab_rows = tab_words[0].rearrange("p t i -> p (t i)").bitcast(I32)
        nc.sync.dma_start(out=tab_codes[:, :EARLY_COLUMNS], in_=tab_rows[:, :EARLY_COLUMNS])
        offsets = keep.tile([P, S // 16], U16, name="offsets")
        nc.sync.dma_start(offsets[:], offs)

        tab_plane = sbuf([P, T // 4], I32, "tab_plane")
        nc.vector.memset(tab_plane[:], 0)
        first_rows = sbuf([P, PASS // 4], I32, "first_rows")
        nc.vector.memset(first_rows[:], 0)
        later_rows = sbuf([P, (H - PASS) // 4], I32, "later_rows")
        nc.vector.memset(later_rows[:], 0)
        wd_plane = sbuf([P, R_BLOCKS, N // 4], I32, "wd_plane")
        nc.vector.memset(wd_plane[:], 0)
        warm = keep.tile([P, 2], F32, name="warm")
        nc.vector.memset(warm[:, 0:1], 0.0)
        nc.scalar.activation(out=warm[:, 1:2], in_=warm[:, 0:1], func=SILU)

        load_scale_rows(nc.sync, tab_plane, tab_scales[0].bitcast(I32))
        nc.sync.dma_start(out=tab_codes[:, EARLY_COLUMNS:], in_=tab_rows[:, EARLY_COLUMNS:])
        load_scale_rows(nc.sync, first_rows, wg_scales[0].bitcast(I32)[:, : PASS // 4])
        first_raw = sbuf([P, PASS // 2], I32, "first_raw")
        nc.sync.dma_start(out=first_raw[:], in_=wg_words[0].bitcast(I32)[:, : PASS // 2])

        def load_up_weight(first, width):
            raw = sbuf([P, PACK * width], F32, f"wu_raw{first}")
            nc.sync.dma_start(
                out=raw[:].rearrange("p (j c) -> p j c", j=PACK),
                in_=wu[:, first : first + width].rearrange("(p j) c -> p j c", j=PACK),
            )
            return raw[:].rearrange("p (j m t) -> p m j t", j=PACK, t=PACK)

        def load_bias(first, end):
            tile = keep.tile([P, end - first, PACK], F32, name=f"bias{first}")
            rows = bg.rearrange("(a p t) -> p a t", p=P, t=PACK)
            nc.sync.dma_start(out=tile[:], in_=rows[:, first:end, :])
            return tile

        cut = PACK * SCALAR_GROUPS
        biases = [load_bias(0, 1)]
        wu_halves = [load_up_weight(0, cut)]
        middle = load_up_weight(cut, PACK * GPSIMD_GROUPS)
        cut = cut + PACK * GPSIMD_GROUPS
        wu_halves.append(load_up_weight(cut, PASS - cut))
        later_raw = sbuf([P, (H - PASS) // 2], I32, "later_raw")
        nc.sync.dma_start(out=later_raw[:], in_=wg_words[0].bitcast(I32)[:, PASS // 2 :])
        wu_halves.append(load_up_weight(PASS, PASS // 2))
        biases.append(load_bias(1, R_BLOCKS))
        load_scale_rows(nc.sync, later_rows, wg_scales[0].bitcast(I32)[:, PASS // 4 :])
        wu_halves.extend(load_up_weight(first, PASS // 2) for first in range(PASS + PASS // 2, H, PASS // 2))
        load_scale_rows(nc.sync, wd_plane, wd_scales.bitcast(I32).rearrange("a q c -> q a c"))
        wd_codes = sbuf([P, R_BLOCKS, N], I32, "wd_codes")
        nc.sync.dma_start(out=wd_codes[:], in_=wd_words.rearrange("a p c i -> p a (c i)").bitcast(I32))
        residual_rows = []
        for n in range(N_TILES):
            g_rows = keep.tile([P, T], F32, name=f"g_rows{n}")
            nc.sync.dma_start(out=g_rows[:], in_=gT[n * P : (n + 1) * P, :])
            residual_rows.append(g_rows)

        def listed(first, end):
            return offsets[:, first // 16 : end // 16]

        def gather_words(first, end):
            codes = sbuf([P, end - first], U32, f"v_codes{first}")
            nc.vector.tensor_copy(codes[:], tab_codes[:].bitcast(U32).indirect(listed(first, end)))
            v_codes[first] = codes

        def token_codes(first, width):
            start = max(key for key in v_codes if key <= first)
            return v_codes[start][:, first - start : first - start + width].bitcast(FP8X4)

        def gather_scales(name, first, end):
            plane = sbuf([P, end - first], U8, name)
            nc.vector.tensor_copy(plane[:], tab_plane[:].bitcast(U8).indirect(listed(first, end)))
            return plane

        def token_scales(first, width):
            if first < EARLY_SCALES:
                return early_scales[:, first : first + width]
            return late_scales[:, first - EARLY_SCALES : first - EARLY_SCALES + width]

        def dealt(ordered, raw):
            return {
                "out": ordered.rearrange("p (a t m) -> p a t m", t=PACK, m=P),
                "in_": raw.rearrange("p (a m t) -> p a t m", t=PACK, m=P),
            }

        def deal_words(a, raw):
            codes = sbuf([P, PASS], U16, f"wg_codes{a}")
            nc.scalar.copy(**dealt(codes[:], raw.bitcast(U16)))
            return codes[:]

        def deal_plane(engine, a, rows):
            plane = sbuf([P, PASS], U8, f"wg_plane{a}")
            engine.tensor_copy(**dealt(plane[:], rows.bitcast(U8)))
            wg_planes.append(plane[:])

        def slots_tile(name, groups):
            tile = sbuf([P, PACK * groups * PACK], BF16, name)
            return tile, tile[:].rearrange("p (t m j) -> p m j t", t=PACK, j=PACK)

        def round_on_gpsimd(dst, src):
            walk = "p m j t -> p m t j"
            nc.gpsimd.tensor_scalar(dst.rearrange(walk), src.rearrange(walk), 1.0, 0.0, MULT, ADD)

        def quantize(name, parts, tag=None):
            codes = sbuf([P, PASS], U32, f"{name}_codes", tag)
            plane = sbuf([P, PASS], U8, f"{name}_plane")
            first = 0
            for part in parts:
                cols = slice(first, first + part.shape[1] // PACK)
                nc.vector.quantize_mx(out=codes[:, cols].bitcast(FP8X4), scales=plane[:, cols], in_=part)
                first = cols.stop
            return codes, plane

        def wide_bank(name="wide_bank"):
            return psum.tile([P, HALF], F32, name=name, bufs=4)

        def gate_pass(bank, a, h, t, first, width):
            nc.tensor.matmul_mx(
                out=bank,
                lhsT=wg_codes[a].bitcast(U8)[:, 2 * P * t : 2 * P * (t + 1)].bitcast(FP4X4),
                lhsT_scale=wg_planes[a][:, P * t : P * (t + 1)],
                rhs=token_codes(h * HALF + first, width),
                rhs_scale=token_scales(h * HALF + first, width),
                start=True,
                stop=True,
            )

        def silu(gated, bank, a, t):
            nc.scalar.activation(out=gated, in_=bank, func=SILU, bias=biases[min(a, 1)][:, max(a - 1, 0), t : t + 1])

        def gate(a, h, first=0, end=HALF):
            width = end - first
            gated = sbuf([P, PACK, width], F32, f"gated{a}_{h}_{first}")
            if width == CHUNK:
                bank = wide_bank()
                for t in range(PACK):
                    gate_pass(bank[:, t * CHUNK : (t + 1) * CHUNK], a, h, t, first, CHUNK)
                for t in range(PACK):
                    silu(gated[:, t, :], bank[:, t * CHUNK : (t + 1) * CHUNK], a, t)
            else:
                for t in range(PACK):
                    if (a, h) == (0, 0) and t < PACK // 2:
                        for lo, name in ((0, "wide_bank"), (QUARTER, "up_bank")):
                            bank = wide_bank(name)
                            gate_pass(bank[:, :QUARTER], a, h, t, lo, QUARTER)
                            silu(gated[:, t, lo : lo + QUARTER], bank[:, :QUARTER], a, t)
                        continue
                    bank = wide_bank("up_bank" if (a, h, t) == (0, 1, 0) else "wide_bank")
                    starts = list(range(first, end, QUARTER))
                    for lo in starts if t < PACK // 2 else reversed(starts):
                        gate_pass(bank[:, lo - first : lo - first + QUARTER], a, h, t, lo, QUARTER)
                    silu(gated[:, t, :], bank[:, :width], a, t)
            return [gated[:, :, c : c + CHUNK] for c in range(0, width, CHUNK)]

        def up(a, h, c):
            bank = psum.tile([P, PACK, CHUNK], F32, name="up_bank", bufs=4)
            for t in range(PACK) if c == 0 else reversed(range(PACK)):
                nc.tensor.matmul_mx(
                    out=bank[:, t, :],
                    lhsT=wu_mx[a][0][:, P * t : P * (t + 1)].bitcast(FP8X4),
                    lhsT_scale=wu_mx[a][1][:, P * t : P * (t + 1)],
                    rhs=token_codes(h * HALF + c * CHUNK, CHUNK),
                    rhs_scale=token_scales(h * HALF + c * CHUNK, CHUNK),
                    start=True,
                    stop=True,
                )
            return bank

        def products(a, h, gated, first_chunk=0):
            hidden = sbuf([P, (CHUNKS - first_chunk) * PASS], BF16, f"hidden{a}_{h}")
            for c in range(first_chunk, CHUNKS):
                place = (c - first_chunk) * PASS
                nc.vector.tensor_tensor(
                    out=hidden[:, place : place + PASS].rearrange("p (g i t) -> p g t i", i=RUN, t=PACK),
                    in0=up(a, h, c)[:].rearrange("p t (g i) -> p g t i", i=RUN),
                    in1=gated[c].rearrange("p t (g i) -> p g t i", i=RUN),
                    op=MULT,
                )
            return hidden

        def copy_first_up(a, h):
            copied = sbuf([P, CHUNK, PACK], F32, f"up_copied{a}")
            nc.scalar.copy(out=copied[:], in_=up(a, h, 0)[:].rearrange("p t c -> p c t"))
            return copied

        def product_on_gpsimd(a, copied, gated):
            lead = sbuf([P, PASS], BF16, f"lead{a}")
            nc.gpsimd.tensor_tensor(
                out=lead[:].rearrange("p (c t) -> p c t", t=PACK),
                in0=copied[:],
                in1=gated[0].rearrange("p t c -> p c t"),
                op=MULT,
            )
            return lead

        def down(h, n):
            bank = wide_bank()
            for a in range(R_BLOCKS):
                nc.tensor.matmul_mx(
                    out=bank[:],
                    lhsT=wd_codes[:, a, P * n : P * (n + 1)].bitcast(FP8X4),
                    lhsT_scale=wd_plane[:, a, :].bitcast(U8)[:, P * n : P * (n + 1)],
                    rhs=h_mx[h][a][0][:].bitcast(FP8X4),
                    rhs_scale=h_mx[h][a][1][:],
                    start=(a == 0),
                    stop=(a == R_BLOCKS - 1),
                )
            product = keep.tile([P, HALF], F32, name=f"product{h}_{n}")
            nc.scalar.copy(out=product[:], in_=bank[:])
            return product

        def finish(h, n, product):
            result = keep.tile([P, HALF], F32, name=f"result{h}_{n}")
            cuts = (0, HALF - LAST_PIECE, HALF) if (h, n) == (1, N_TILES - 1) else (0, HALF)
            for first, end in zip(cuts, cuts[1:]):
                picked = residual_rows[n][:].indirect(listed(h * HALF + first, h * HALF + end))
                nc.vector.tensor_tensor(result[:, first:end], picked, product[:, first:end], ADD)
                nc.sync.dma_start(
                    out=out[n * P : (n + 1) * P, h * HALF + first : h * HALF + end], in_=result[:, first:end]
                )

        wg_codes = [deal_words(0, first_raw[:])]
        early_scales = gather_scales("early_scales", 0, EARLY_SCALES)
        v_codes = {}
        gather_words(0, QUARTER)
        wg_planes = []
        deal_plane(nc.vector, 0, first_rows[:])
        gather_words(QUARTER, HALF)
        late_scales = gather_scales("late_scales", EARLY_SCALES, S)
        gather_words(HALF, S)
        slots, dst = slots_tile("wu_slots0", P)
        nc.scalar.copy(out=dst[:, :SCALAR_SHARE], in_=wu_halves[0][:, :SCALAR_SHARE])
        round_on_gpsimd(dst[:, SCALAR_SHARE:SCALAR_GROUPS], wu_halves[0][:, SCALAR_SHARE:])
        rest = SCALAR_GROUPS + GPSIMD_GROUPS
        round_on_gpsimd(dst[:, SCALAR_GROUPS:rest], middle)
        for pair in (slice(0, 2), slice(2, 4)):
            nc.vector.tensor_copy(out=dst[:, rest:, :, pair], in_=wu_halves[1][:, :, :, pair])
        wu_mx = [quantize("wu0", [slots[:, : 2 * PASS], slots[:, 2 * PASS :]])]
        later_codes = sbuf([P, H - PASS], U16, "later_codes")
        nc.vector.tensor_copy(**dealt(later_codes[:], later_raw[:].bitcast(U16)))
        wg_codes.extend([later_codes[:, :PASS], later_codes[:, PASS:]])
        h_mx = ([], [])

        def whole(a, h, hidden, tag=None):
            h_mx[h].append(quantize(f"h{a}_{h}", [hidden[:]], tag))

        def shared_unit(a, lead, hidden):
            h_mx[1].append(quantize(f"h{a}_1", [lead[:], hidden[:, :PASS], hidden[:, PASS:]]))

        gated = [gate(0, 0), gate(0, 1)]
        slots, dst = slots_tile("wu_slots1", P)
        round_on_gpsimd(dst[:, : P // 2], wu_halves[2])
        nc.scalar.copy(out=dst[:, P // 2 :], in_=wu_halves[3])
        deal_plane(nc.gpsimd, 1, later_rows[:, : PASS // 4])
        lower, dst = slots_tile("wu_lower2", P // 2)
        round_on_gpsimd(dst, wu_halves[4])
        hidden = [products(0, h, gated[h]) for h in range(2)]
        wu_mx.append(quantize("wu1", [slots[:]]))
        whole(0, 0, hidden[0])
        whole(0, 1, hidden[1], "wu_raw1024")

        gated = [gate(1, 0)]
        deal_plane(nc.gpsimd, 2, later_rows[:, PASS // 4 :])
        upper, dst = slots_tile("wu_upper2", P // 2)
        round_on_gpsimd(dst, wu_halves[5])
        gated.append(gate(1, 1))
        hidden = products(1, 0, gated[0])
        copied = copy_first_up(1, 1)
        parts = [tile[:, t * 256 : (t + 1) * 256] for t in range(PACK) for tile in (lower, upper)]
        wu_mx.append(quantize("wu2", parts))
        whole(1, 0, hidden)

        lead = product_on_gpsimd(1, copied, gated[1])
        hidden = products(1, 1, gated[1], first_chunk=1)
        gated = [gate(2, 0), gate(2, 1, 0, CHUNK)]
        shared_unit(1, lead, hidden)

        lead = product_on_gpsimd(2, copy_first_up(2, 1), gated[1])
        gated[1].extend(gate(2, 1, CHUNK, QUARTER) + gate(2, 1, QUARTER, HALF))
        whole(2, 0, products(2, 0, gated[0]))
        shared_unit(2, lead, products(2, 1, gated[1], first_chunk=1))

        for h in range(2):
            for n in range(N_TILES):
                finish(h, n, down(h, n))
